import numpy as np, ml_dtypes
CORES = [13,21,141,149]
N = 4
BF = ml_dtypes.bfloat16
S, L, R, B, CAP = 4, 256, 3, 1152, 64
A, W = S * L, B + R * L
def parts(rng):
    x = rng.integers(0, 256, (N, 8, 16, B)); k = rng.integers(0, B, (N, 8, 16, B))
    head = rng.integers(0, B, (N, 8, 6, 64)); clan = rng.integers(0, 64, (N, 8, 1, B))
    k[:, :, :6] = np.where(rng.random((N, 8, 6, B)) < 0.35, np.take_along_axis(head, np.repeat(clan, 6, axis=2), 3), k[:, :, :6])
    return x, k, rng.integers(800, 1201, (N, 8, R)), rng.integers(0, 256, (N, 8, 16, R))
def pack(x, k, th, w):
    return {"xf": np.ascontiguousarray(x.reshape(N, 128, B)).astype(np.float32).astype(BF), "kin": np.ascontiguousarray(k.reshape(N, 128, B)).astype(np.int32),
            "th": np.ascontiguousarray(th).astype(np.int32), "w": np.ascontiguousarray(w.reshape(N, 128, R)).astype(np.int32)}
def setup_inputs(rng):
    return pack(*parts(rng))
def setup_inputs_spread(rng):
    x, k, th, w = parts(rng)
    size = np.exp2(8 * rng.random((N, 8, 1, B))) * (rng.random((N, 8, 1, B)) > 0.0625)
    x = np.minimum((size * rng.random(x.shape)).astype(np.int64), 255)
    few = np.minimum((B * rng.random(k.shape) ** rng.choice(np.array([1.0, 2.0, 4.0]), (N, 8, 1, 1))).astype(np.int64), B - 1)
    k = np.where(rng.random(k.shape) < 0.5, few, k)
    th = np.minimum(np.exp2(4 + 8 * rng.random(th.shape)).astype(np.int64), 4095)
    w = np.minimum((np.exp2(8 * rng.random((N, 8, 1, R))) * rng.random(w.shape)).astype(np.int64), 255)
    return pack(x, k, th, w)
def setup_inputs_ends(rng):
    x, k, th, w = parts(rng)
    kind = rng.integers(0, 3, (N, 8, 1, B)); x = 255 * np.where(kind == 2, rng.integers(0, 2, x.shape), kind)
    loose = rng.random((N, 8, 1, B)) < 0.2; loose[..., 0] = True; loose[..., B - 1] = True
    k[:, 7] = rng.integers(0, B - 32, (N, 16, B))
    end = (B - 1) * rng.integers(0, 2, k.shape); k = np.where(loose, k, end)
    top = np.arange(B - 32, B - 2); top = top[(top & (S - 1)) != 0][-16:]; last = S * (L - 1) + np.arange(R)
    kg, xg = k[:, 7], x[:, 7]
    mid = S * np.arange(CAP // 2, L - 1) + 1; xg[:, :, mid] = 255
    kg[:, :, last] = B - 2; xg[:, :, last] = 0; xg[:, :, top] = 255; kg[:, :, top] = end[:, 7][:, :, top]
    for q in range(N): kg[q, :, B - 2] = rng.permutation(top)
    th = 4095 * rng.integers(0, 2, th.shape); th[:, 7] = 4095 * ((np.arange(R) + 1) & 1)
    w = 255 * rng.integers(0, 2, w.shape); w[:, 7] = 255
    return pack(x, k, th, w)
def setup_inputs_corners(rng):
    x, k, th, w = parts(rng); i = np.arange(L); v = S * i; u = v + 1; mm = v + 2; own = np.arange(B)
    z = rng.integers(0, 6, (N, 4, 16, B)); k[:, 1::2] = np.where(z == 0, 0, np.where(z == 1, B - 1, np.where(z == 2, own, k[:, 1::2])))
    e = k[..., mm]; k[..., mm] = e + ((e & (S - 1)) == 1)
    th = rng.choice(np.array([0, 1, 700, 1000, 1100, 4095]), th.shape); w = rng.choice(np.array([0, 1, 128, 255]), w.shape)
    for q in range(N):
        for g in range(8):
            F = int(rng.choice(np.array([0, 1, CAP - 1, CAP, CAP + 1, L])))
            if q == 0: F = (0, 1, CAP - 1, CAP, CAP + 1, L, CAP, L)[g]
            must = q == 0 and g == 3
            lose = np.zeros(L, bool); o = rng.permutation(L)
            if must: o = np.concatenate([np.array([0]), 1 + rng.permutation(L - 2), np.array([L - 1])])
            lose[o[:F]] = True
            if q == N - 1 and g == 7: lose = i >= L - CAP
            t0 = int(rng.choice(np.array([1, 17, 300, 2399]))); how = rng.integers(0, 4, L)
            if must: how[0] = 1
            far0 = np.where(lose & (how == 3), t0, np.where(rng.random(L) < 0.5, t0 - 1, rng.integers(0, t0, L)))
            kg, xg = k[q, g], x[q, g]; base = rng.integers(0, 100, (16, L))
            xg[:, v] = base; xg[:, mm] = base + far0 // 16 + (np.arange(16)[:, None] < (far0 & 15))
            src = np.nonzero(~lose | (how == 3))[0]; at = np.searchsorted(src, i); goal = mm.copy()
            named = lose & (how == 2) & (at > 0); none = lose & ((how == 0) | ((how == 2) & (at == 0))); blood = lose & (how == 1)
            bl, wl = np.nonzero(blood)[0], np.nonzero(~lose)[0]
            if must: bl, wl = bl[1:], wl[:-1]
            pairs = min(len(bl), len(wl)); bl = bl[np.argsort(rng.random(len(bl)))[:pairs]]; wl = wl[np.argsort(rng.random(len(wl)))[:pairs]]
            ok = bl < wl; bl, wl = bl[ok], wl[ok]
            if must: bl, wl = np.append(bl, 0), np.append(wl, L - 1)
            goal[wl] = mm[bl]; xg[:, v[wl]] = xg[:, goal[wl]]
            j = (rng.random(L) * at).astype(np.int64)
            if np.any(named):
                goal[named] = goal[src[j[named]]]; xg[:, v[named]] = xg[:, goal[named]]
            goal[none] = np.where(rng.random(L) < 0.5, v, S * rng.integers(0, L, L))[none]
            kg[:, v] = u; kg[:, u] = goal; row = rng.integers(0, 6, L); kg[row[blood], mm[blood]] = u[blood]
            th[q, g, 0] = t0
    return pack(x, k, th, w)
def setup_inputs_ties(rng):
    x, k, th, w = parts(rng); x = rng.integers(0, 3, x.shape); x[:, 1::2] = rng.integers(0, 2, (N, 4, 16, B))
    crowd = rng.integers(0, B, (N, 8, 48)); j = rng.integers(0, 48, (N, 8, 16 * B))
    c = np.take_along_axis(crowd, j, 2).reshape(k.shape); m = rng.random(k.shape) < 0.6; m[:, 1::2] = False; k = np.where(m, c, k)
    th = rng.integers(3, 13, th.shape); one = int(rng.integers(0, 8)); x[:, one] = 255; th[:, one] = rng.integers(0, 2, (N, R))
    return pack(x, k, th, w)
def court(rng, xg, kg, t, goal, d):
    v = S * np.arange(L) + t; u = S * rng.permutation(L) + 3; base = rng.integers(0, 240, (16, L))
    xg[:, v] = base; xg[:, goal] = base + d // 16 + (np.arange(16)[:, None] < (d & 15))
    kg[8, v] = u; kg[(8 + t) & 15, u] = goal
def setup_inputs_turns(rng):
    x, k, th, w = parts(rng); own = np.arange(B); o = int(rng.integers(0, N)); towns = rng.permutation(8)[:4]; row = np.arange(16)[:, None]
    for full in range(2):
        q = (o + full) % N; t = 2 - full
        k[q, :, :6] = (k[q, :, :6] & -2) | (own & 1)
        count = 16 * rng.integers(1, 5, 8); count[int(rng.integers(0, 8))] += 15
        if full: count[:] = L
        th[q, :, 1] = 0
        for g in range(8):
            a, b = int(rng.integers(17, 100)), int(rng.integers(17, 100))
            d = np.where(rng.permutation(L) < count[g], rng.integers(0, a, L), a + rng.integers(0, 15, L))
            court(rng, x[q, g], k[q, g], 0, S * rng.permutation(L) + 3, d)
            d = np.where(rng.random(L) < 0.5, b - 1, b + rng.integers(0, 15, L))
            court(rng, x[q, g], k[q, g], t, S * rng.permutation(L) + 1 + full, d)
            th[q, g, 0] = a; th[q, g, t] = b
    for j in range(2, N):
        q = (o + j) % N
        for g in towns:
            xg, kg = x[q, g], k[q, g]
            high = int(rng.integers(200, 235)); y = rng.integers(0, 21, (8, B))
            xg[0::2] = high + y; xg[1::2] = high - y; xg += row < rng.integers(0, 16, B)
            low = int(rng.integers(20, 50)); y = rng.integers(0, 20, (8, L)); tight = np.zeros((16, L), np.int64)
            tight[0::2] = low + y; tight[1::2] = low - y; tight += row < rng.integers(0, 4, L)
            loose = np.clip(rng.integers(0, 71, L) + rng.integers(-8, 9, (16, L)), 0, 70)
            xg[:, S * np.arange(L)] = np.where(rng.random(L) < 0.5, tight, loose)
            kg += (kg & (S - 1)) == 0
            th[q, g, 0] = 16 * (high - low)
    return pack(x, k, th, w)
def check_inputs(d):
    bad = []
    for a, lo, hi in (("xf", 0, 255), ("kin", 0, B - 1), ("th", 0, 4095), ("w", 0, 255)):
        b = np.asarray(d[a]).astype(np.float64)
        if not (np.min(b) >= lo and np.max(b) <= hi): bad.append("range of " + a)
        if np.any(b != np.floor(b)): bad.append("whole numbers in " + a)
    return bad
def pick(a, ix):
    return np.stack([np.stack([np.take(a[q, g], ix[q, g], axis=1) for g in range(8)]) for q in range(N)])
def score(xc, xv):
    return np.add.reduce(np.abs(xc - xv[:, :, :, None, :]), axis=2)
def reference(xf, kin, th, w):
    X = np.zeros((N, 8, 16, W), np.int32); X[..., :B] = xf.astype(np.float32).reshape(N, 8, 16, B).astype(np.int32)
    K = np.zeros((N, 8, 16, W), np.int32); K[..., :B] = kin.reshape(N, 8, 16, B)
    wt = w.astype(np.int32).reshape(N, 8, 16, R); lane = np.arange(L, dtype=np.int32); last = np.zeros(N, np.int32)
    qa = np.arange(N).reshape(N, 1, 1, 1); ga = np.arange(8).reshape(1, 8, 1, 1); ka = np.arange(16).reshape(1, 1, 16, 1)
    for t in range(R):
        v = S * lane + t; n = B + L * t + lane; kv = K[..., v]; xv = X[..., v]
        c = K[qa, ga, (ka + t) & 15, kv]
        bar = ((c & (S - 1)) == t) | np.any(pick(K[:, :, :6], c) == kv[:, :, :6, None, :], axis=2)
        s = np.where(bar, 1000000, score(pick(X, c), xv))
        best = np.argmin(s, axis=2); low = np.min(s, axis=2); some = low < 1000000
        m = np.where(some, np.take_along_axis(c, best[:, :, None, :], 2)[:, :, 0], -1 - lane)
        taken = np.any((m[..., :, None] == m[..., None, :]) & (lane[:, None] > lane[None, :]), axis=3)
        wed = some & ~taken & (low < th[:, :, t][:, :, None] + (last & 15)[:, None, None])
        last = np.add.reduce(np.add.reduce(wed.astype(np.int32), axis=2), axis=1)
        ms = np.where(wed, m, v); km = pick(K, ms); xm = pick(X, ms)
        vb = np.broadcast_to(v, (N, 8, 1, L)); nb = np.broadcast_to(n, (N, 8, 1, L))
        child = np.concatenate([vb, ms[:, :, None, :], kv[:, :, 0:2], km[:, :, 0:2], nb, nb, kv[:, :, 7:8], km[:, :, 9:16]], axis=2)
        lost = (~wed).astype(np.int32); ask = ~wed & (np.add.accumulate(lost, axis=2) - lost < CAP)
        far = 1 + t % (N - 1); Kq = np.roll(K, -far, axis=0); Xq = np.roll(X, -far, axis=0)
        a = np.add.reduce(wt[..., t][..., None] * xv, axis=2) & (A - 1)
        cx = pick(Xq, pick(Kq, a)); bq = np.argmin(score(cx, xv), axis=2)
        near = np.take_along_axis(cx, bq[:, :, None, None, :], 3)[:, :, :, 0]
        X[..., n] = np.where(wed[:, :, None], (xv + xm) >> 1, np.where(ask[:, :, None], near, xv))
        K[..., n] = np.where(wed[:, :, None], child, kv)
        K[:, :, 6, v] = np.where(wed, m, kv[:, :, 6]); K[:, :, 7, v] = np.where(wed, n, kv[:, :, 7]); K[:, :, 9 + t, v] = np.where(ask, n, kv[:, :, 9 + t])
        qi, gi, li = np.nonzero(wed); mi = m[qi, gi, li]; K[qi, gi, 6, mi] = v[li]; K[qi, gi, 7, mi] = n[li]
    return {"yk": K.reshape(N, 128, W).astype(np.float32), "yx": np.ascontiguousarray(X[..., B:]).reshape(N, 128, R * L).astype(np.float32).astype(BF)}

@@ -1,0 +1,747 @@
+from concourse.bass import DstId, RemoteDMATransfer
+from concourse.mybir import dt, AluOpType, AxisListType, ActivationFunctionType
+
+ALU = AluOpType
+ACT = ActivationFunctionType
+N, B, L, R, W = 4, 1152, 256, 3, 1920
+BIGK = 131072.0
+MAGIC = 12582912.0
+
+F32, BF, F16, I32, U16 = "float32", "bfloat16", "float16", "int32", "uint16"
+_S = {
+    "kin32": (B, I32), "K0f": (B, F32), "Kf": (W, F32), "KC": (W, F32), "X": (W + 64, BF),
+    "XQ0": (B, BF), "XQ1": (B + L, BF), "XQ2": (B + 2 * L, BF),
+    "D0": (320, F32), "D1": (320, F32), "D2": (320, F32), "DS0": (L, F32), "DS1": (L, F32), "DS2": (L, F32),
+    "aS": (48, U16), "aR0": (16, U16), "aR1": (16, U16), "aR2": (16, U16), "aI": (48, I32), "aJ": (48, I32),
+    "w32": (4, I32), "th32": (4, I32), "thf": (4, F32),
+    "inp": (160, F32), "inn": (320, F32), "ing": (128, F32), "pI": (8, I32), "col": (64, F32), "mask": (16, F32),
+    "E0": (160, BF), "E1": (160, BF), "Id": (128, BF), "nId": (128, BF), "Zm": (128, BF), "Big": (144, BF), "Bigf": (144, F32),
+    "BigC": (144, BF), "Big6": (144, BF), "Big7": (144, BF), "BigW": (432, BF), "BO": (128, BF), "BOd": (128, BF), "BOo": (128, BF),
+    "P1a": (128, BF), "P1b": (128, BF), "P2a": (128, F32), "P2b": (128, F32), "Pm1": (128, BF), "Pm6": (128, BF), "M05": (128, BF),
+    "o16": (128, F32), "s8": (128, F32), "lP15": (16, U16), "lCol": (16, U16), "lPerm": (16, U16), "tl": (48, F32),
+    "diag": (256, BF), "kcon": (256, BF), "pw": (32, F32), "thrB": (256, F32), "iB": (256, BF), "c3": (256, BF), "one": (320, BF),
+    "pos": (64, F16), "seg": (64, F32), "vT": (48, F32), "scol": (8, F32), "junk": (320, BF),
+    "kvs": (768, F16), "kvd": (768, F16), "tr": (768, F32), "off1": (768, U16), "off2": (768, U16), "xvS": (960, BF), "xvm": (256, F32),
+    "G": (8192, F16), "Gf": (2048, F32), "Cq": (8192, BF), "xc": (8192, BF), "ad": (8192, BF),
+    "key1": (576, F32), "c1": (576, F32), "key2": (288, F32), "c2": (288, F32), "ta": (256, F32), "tb": (256, F32), "tc": (192, F32),
+    "td": (96, F32), "te": (96, F32), "km": (16, F32), "mT": (16, F32), "mS": (16, F32), "iv": (16, F32), "nc": (16, F32), "dmv": (16, F32),
+    "Em": (256, F16), "En": (256, BF), "mB": (256, F16), "eq": (4096, BF), "wed": (320, BF), "cum": (320, F32), "Lm": (256, F32), "Fv": (256, BF),
+    "t1": (16, F32), "t2": (16, F32), "msl": (16, U16), "kmz": (256, F32), "cvn": (256, F32), "cv2": (256, F16), "cn": (256, F16),
+    "prC": (256, F16), "prV": (256, F16), "sm": (256, F32), "sy": (256, F32), "acc": (8, F32), "lan": (8, U16), "Dc": (64, U16),
+    "xvc": (64, BF), "xq": (1024, BF), "rs": (64, F32), "ri": (8, I32), "rj": (8, I32), "rl": (8, U16), "near": (64, BF),
+    "zi": (8, I32), "thr": (8, F32),
+}
+_S.update({"tf": (96, F16), "tc": (192, F16), "kC": (768, F32), "jv": (640, BF), "DD": (768, BF), "hPm6": (128, BF), "hId": (128, BF), "mh": (256, BF),
+           "o16": (128, BF), "cum": (320, BF), "sm": (256, BF)})
+del _S["Lm"], _S["xvm"]
+POOL = {}
+for _p, _d, _names in (("poolf", F32, "km mT mS iv nc dmv t1 t2 acc thr scol td te pw tl vT seg rs"), ("pooli", I32, "aI aJ ri rj zi pI"),
+                       ("poolu", U16, "lP15 lCol lPerm msl lan rl Dc")):
+    _at = 0
+    for _n in _names.split():
+        POOL[_n] = (_p, _at)
+        _at += (_S[_n][0] + 15) // 16 * 16
+    _S[_p] = (_at, _d)
+SCRATCH = {k: ("sbuf", [128, v[0]], v[1]) for k, v in _S.items() if k not in POOL}
+SCRATCH["aq"] = ("sbuf", [128, 4, 256], BF)
+for _b in range(8):
+    SCRATCH["P%d" % _b] = ("psum", [128, 512], F32)
+NDMA = 40
+FLOWS = ["xs0", "xs1", "xs2", "a0", "a1", "a2", "d0", "d1", "d2", "xn01", "xn02", "xn12"]
+SEMAPHORES = ["sV", "sA", "sP", "sG", "sent"] + ["m%d" % i for i in range(NDMA)] + FLOWS + ["h" + f for f in FLOWS]
+SIZE = {F32: 4, BF: 2, F16: 2, I32: 4, U16: 2}
+A_ON_SCALAR = {(0, 12): 0, (0, 8): 1024, (1, 9): 0, (2, 9): 1024}
+COUNT_ON_V, KM_ON_V, XQ_ON_A = [2], [2], [0, 1]
+CYC = 0.83e-3 * 1.25
+PEC = 0.42e-3 * 1.25
+
+
+def flows(T):
+    f = {}
+    for t in range(R):
+        f["xs%d" % t] = (t, "ans", ("X", 0, B), ("XQ%d" % t, 0, B))
+        f["a%d" % t] = (t, "ask", ("aS", 16 * t, 16 * t + 16), ("aR%d" % t, 0, 16))
+        f["d%d" % t] = (t, "ans", ("DS%d" % t, 0, L), ("D%d" % t, 0, L))
+    for s, t in ((0, 1), (0, 2), (1, 2)):
+        f["xn%d%d" % (s, t)] = (t, "ans", ("X", B + L * s, B + L * s + L), ("XQ%d" % t, B + L * s, B + L * s + L))
+    return f
+
+
+def route(T, topo, r, name):
+    t, kind = flows(T)[name][:2]
+    far = 1 + t % (N - 1)
+    q = (r + far) % N if kind == "ask" else (r - far) % N
+    src, dst = T.cores[r], T.cores[q]
+    if topo.may_write(src, dst):
+        return dst, None
+    can = [c for c in topo.cores_of(src) if c != src and T.rank_of(c) is None and topo.may_write(c, dst)]
+    same = [c for c in can if topo.die(c) == topo.die(src)]
+    other = [c for c in can if topo.die(c) != topo.die(src)]
+    can = same + other
+    if name.startswith("xs"):
+        return dst, (same[0] if t == 0 else other[0])
+    return dst, same[-1]
+
+
+def nbits(m):
+    return bin(m).count("1")
+
+
+RELAY_ORDER = ["xs0", "a0", "a2", "xs2", "d0", "xn02", "d2", "xn12", "xs1", "a1", "d1", "xn01"]
+
+
+def relay_program(g, core, T, topo):
+    fl = flows(T)
+    sent = 0
+    for name in RELAY_ORDER:
+        for r in range(N):
+            dst, rel = route(T, topo, r, name)
+            if rel != core:
+                continue
+            nm, lo, hi = fl[name][3]
+            g.wait_ge(T.sem["h" + name], nbits(topo.mask(T.cores[r], core)))
+            rid, pid = topo.addr(dst, core)
+            m = topo.mask(core, dst)
+            g.remote_dma(T[nm][:, lo:hi], T[nm][:, lo:hi], T.sem[name], T.sem.sent, pid, rid, m)
+            sent += nbits(m)
+    if sent:
+        g.wait_ge(T.sem.sent, sent)
+
+
+def rank_program(g, core, T, topo):
+    rank = T.rank_of(core)
+    if rank is None:
+        return relay_program(g, core, T, topo)
+    ops = []
+    last = {}
+    Q = {"V": g.vector, "A": g.scalar, "P": g.tensor, "G": g, "S": g.sync}
+
+    def a(nm, lo=0, hi=None, st=1):
+        if hi is None:
+            hi = 512 if nm[0] == "P" and nm[1:].isdigit() else _S[nm][0]
+        if nm in POOL:
+            nm, lo, hi = POOL[nm][0], lo + POOL[nm][1], hi + POOL[nm][1]
+        ap = T[nm][:, lo:hi] if st == 1 else T[nm][:, lo:hi:st]
+        n = len(range(lo, hi, st))
+        if nm[0] == "P" and nm[1:].isdigit():
+            return {"ap": ap, "r": [(nm, 0, 512)], "n": n, "sz": 4, "ps": True}
+        return {"ap": ap, "r": [(nm, lo, lo + (n - 1) * st + 1)], "n": n, "sz": SIZE[_S[nm][1]], "ps": False}
+
+    def ind(win, off):
+        return {"ap": win["ap"].indirect(off["ap"]), "r": win["r"] + off["r"], "n": 16 * off["n"], "sz": win["sz"], "ps": False,
+                "win": win["r"], "off": off["r"]}
+
+    def op(eng, fn, reads, writes, cost, kind="c", after=(), wait=None):
+        i = len(ops)
+        deps = set(after)
+        acc = []
+        for x in reads:
+            for r_ in x["r"]:
+                acc.append((r_, x["ps"]))
+        for x in writes:
+            if "win" in x:
+                acc += [(r_, True) for r_ in x["win"]] + [(r_, False) for r_ in x["off"]]
+            else:
+                acc += [(r_, True) for r_ in x["r"]]
+        for (nm, lo, hi), wr in acc:
+            for (l2, h2, j, w2) in last.get(nm, []):
+                if l2 < hi and lo < h2 and (wr or w2):
+                    deps.add(j)
+        for (nm, lo, hi), wr in acc:
+            lst = last.setdefault(nm, [])
+            if wr:
+                lst[:] = [e for e in lst if not (lo <= e[0] and e[1] <= hi)]
+            lst.append((lo, hi, i, wr))
+        deps.discard(i)
+        ops.append({"e": eng, "fn": fn, "deps": deps, "cost": cost, "kind": kind, "wait": wait})
+        return i
+
+    def vcost(ins, out, two=False):
+        n = out["n"]
+        if "win" in out:
+            return 0.05 + n * 3.8 * CYC
+        if any("win" in x for x in ins):
+            return 0.05 + n * 1.56 * CYC
+        rate = 2.0 if two else (0.5 if all(x["sz"] == 2 for x in ins + [out]) else 1.0)
+        return 0.04 + max(64, n * rate) * CYC
+
+    def val(s):
+        return s["ap"] if isinstance(s, dict) else s
+
+    def cols(*s):
+        return [x for x in s if isinstance(x, dict)]
+
+    def copy(o, i):
+        return op("V", lambda q: q.tensor_copy(o["ap"], i["ap"]), [i], [o], vcost([i], o))
+
+    def tt(o, i0, i1, f):
+        return op("V", lambda q: q.tensor_tensor(o["ap"], i0["ap"], i1["ap"], f), [i0, i1], [o],
+                  vcost([i0, i1], o, not (i0["ps"] or i1["ps"])))
+
+    def ts(o, i, s1, f0, s2=None, f1=None):
+        if f1 is None:
+            fn = lambda q: q.tensor_scalar(o["ap"], i["ap"], val(s1), None, f0)
+        else:
+            fn = lambda q: q.tensor_scalar(o["ap"], i["ap"], val(s1), val(s2), f0, f1)
+        return op("V", fn, [i] + cols(s1, s2), [o], vcost([i], o))
+
+    def red(o, i):
+        return op("V", lambda q: q.tensor_reduce(o["ap"], i["ap"], AxisListType.X, ALU.add), [i], [o], 0.04 + max(64, i["n"]) * CYC)
+
+    def mset(o, c):
+        return op("V", lambda q: q.memset(o["ap"], c), [], [o], vcost([], o))
+
+    def scan(o, d0, d1, init, f0, f1):
+        return op("V", lambda q: q.tensor_tensor_scan(o["ap"], d0["ap"], d1["ap"], init, f0, f1), [d0, d1], [o], vcost([d0, d1], o))
+
+    def act(o, i, f=ACT.Identity, bias=0.0, scale=1.0, accum=None):
+        if accum is None:
+            fn = lambda q: q.activation(o["ap"], i["ap"], f, val(bias), val(scale))
+        else:
+            fn = lambda q: q.activation(o["ap"], i["ap"], f, val(bias), val(scale), accum_out=accum["ap"])
+        c = 0.065 + (i["n"] * 1.56 if "win" in i else max(64, i["n"])) * CYC
+        return op("A", fn, [i] + cols(bias, scale), [o] + cols(accum), c)
+
+    def mm(lst, first=True, final=True):
+        def fn(q):
+            ins = None
+            for j, (o, l_, r_) in enumerate(lst):
+                ins = q.matmul(o["ap"], l_["ap"], r_["ap"], first and j == 0, final and j == len(lst) - 1)
+            return ins
+        c = sum(max(64, r_["n"]) * (4 if r_["sz"] == 4 else 1) for o, l_, r_ in lst) * PEC
+        return op("P", fn, [x for e in lst for x in e[1:]], [e[0] for e in lst], c)
+
+    def iota(o, pat, base, cm, flag=True):
+        if flag:
+            fn = lambda q: q.iota(o["ap"], pat, base, cm, allow_small_or_imprecise_dtypes=True)
+        else:
+            fn = lambda q: q.iota(o["ap"], pat, base, cm)
+        return op("G", fn, [], [o], 0.13 + 2 * o["n"] * CYC)
+
+    def dma(eng, oap, iap, reads, writes, nbytes, after=()):
+        return op(eng, lambda q: q.dma_start(oap, iap), reads, writes, 2.0 + nbytes / 150e3, "d", after)
+
+    fl = flows(T)
+    sent = [0]
+
+    def send(name, after=()):
+        t, kind, (sn, sl, sh), (dn, dl, dh) = fl[name]
+        dst, rel = route(T, topo, rank, name)
+        to = dst if rel is None else rel
+        rid, pid = topo.addr(to, core)
+        m = topo.mask(core, to)
+        sem = T.sem[name] if rel is None else T.sem["h" + name]
+        sent[0] += nbits(m)
+        nb = 128 * (sh - sl) * SIZE[_S[sn][1]]
+        s = op("G", lambda q: q.remote_dma(T[dn][:, dl:dh], T[sn][:, sl:sh], sem, T.sem.sent, pid, rid, m), [a(sn, sl, sh)], [], 0.3, "r", after)
+        far = 1 + t % (N - 1)
+        frm = (rank - far) % N if kind == "ask" else (rank + far) % N
+        d2, r2 = route(T, topo, frm, name)
+        cnt = nbits(topo.mask(T.cores[frm] if r2 is None else r2, core))
+        lat = (3.5 + nb / 60e3) * (1 if rel is None else 2)
+        op("X", None, [], [a(dn, dl, dh)], lat, "x", [s], (name, cnt))
+        return s
+
+    def C(j):
+        return a("col", j, j + 1)
+
+    def M(j):
+        return a("mask", j, j + 1)
+
+    dma("S", T.kin32[:, 0:576], T.kin[:, 0:576], [], [a("kin32", 0, 576)], 300e3)
+    dma("A", T.kin32[:, 576:B], T.kin[:, 576:B], [], [a("kin32", 576, B)], 300e3)
+    dma("S", T.X[:, 0:B], T.xf[:, :], [], [a("X", 0, B)], 500e3)
+    dma("A", T.w32[:, 0:3], T.w[:, :], [], [a("w32", 0, 3)], 0)
+    dma("S", T.th32[0:8, 0:3], T.th[:, :], [], [a("th32", 0, 3)], 0)
+
+    iota(a("pI", 0, 1), [[1, 1]], 0, 1, False)
+    iota(a("inp"), [[1, 160]], -16, -1)
+    iota(a("inn"), [[1, 320]], 0, 0)
+    ts(a("pI", 1, 2), a("pI", 0, 1), 15, ALU.bitwise_and)
+    ts(a("pI", 2, 3), a("pI", 0, 1), 112, ALU.bitwise_and)
+    ts(a("pI", 3, 4), a("pI", 0, 1), 16, ALU.bitwise_and)
+    copy(a("col", 0, 3), a("pI", 0, 3))
+    ts(C(3), C(2), 15.0, ALU.add)
+    ts(C(4), a("pI", 3, 4), 0.0625, ALU.mult)
+    ts(C(5), C(4), -1.0, ALU.mult, 1.0, ALU.add)
+    ts(a("E0"), a("inp"), 0.0, ALU.is_equal, C(5), ALU.mult)
+    ts(a("E1"), a("inp"), 0.0, ALU.is_equal, C(4), ALU.mult)
+    ts(a("mask"), a("inn", 0, 16), C(1), ALU.is_equal)
+    ts(a("Big"), a("inn", 0, 144), C(3), ALU.is_equal)
+    ts(C(10), C(1), 16.0, ALU.mult)
+    ts(a("lPerm"), a("inn", 0, 16), C(10), ALU.add)
+    ts(a("Id"), a("inp", 16, 144), 0.0, ALU.is_equal)
+    act(a("nId"), a("Id"), scale=-1.0)
+    act(a("BigC"), a("Big"), scale=BIGK)
+    act(a("Bigf"), a("Big"))
+    iota(a("KC", 0, B), [[0, B // 4], [1, 4]], 0, 0)
+    iota(a("kcon"), [[1, 16], [0, 16]], 0, 0)
+    iota(a("ing"), [[16, 8], [0, 16]], 0, 0)
+
+    def big(nm, a_, base=0):
+        return a(nm, base + 15 - a_, base + 143 - a_)
+
+    def first_lists(t, bank):
+        copy(a("kvs", 256 * t, 256 * t + 256), a("kin32", t, 1024, 4))
+        for bp in range(8):
+            for c in range(2):
+                o = a(bank, 32 * bp + 16 * c, 32 * bp + 16 * c + 16)
+                e = "E%d" % c
+                lst = []
+                for x in range(2):
+                    sh = 16 - 16 * (x - c)
+                    b_ = 2 * bp + x
+                    lst.append((o, a(e, sh, sh + 128), a("kvs", 256 * t + 16 * b_, 256 * t + 16 * b_ + 16)))
+                mm(lst)
+        o, i = a("tr", 256 * t, 256 * t + 256), a(bank, 0, 256)
+        op("V", lambda q: q.transpose(o["ap"], i["ap"]), [i], [o], vcost([i], o))
+        copy(a("off1", 256 * t, 256 * t + 256), ind(o, a("lPerm")))
+
+    first_lists(0, "P6")
+    copy(a("K0f"), a("kin32"))
+    kc_ops = [dma("S", T.KC[16 * g_:16 * g_ + 6, 0:B], T.K0f[16 * g_:16 * g_ + 6, :], [a("K0f"), a("KC", 0, B)], [], 60e3)
+              for g_ in range(8)]
+    last["KC"] = [(0, B, j, True) for j in kc_ops]
+    dma("S", T.Kf[:, 0:B], T.K0f[:, :], [a("K0f")], [a("Kf", 0, B)], 600e3, kc_ops)
+
+    copy(a("col", 11, 14), a("w32", 0, 3))
+    for t in range(R):
+        act(a("BigW", 144 * t, 144 * t + 144), a("Big"), scale=C(11 + t))
+        mm([(a("P7", 16 * t, 16 * t + 16), big("BigW", a_, 144 * t), a("X", 4 * a_ + t, 1024, 64)) for a_ in range(16)])
+    copy(a("aI"), a("P7", 0, 48))
+    ts(a("aJ"), a("aI"), 1023, ALU.bitwise_and)
+    copy(a("aS"), a("aJ"))
+    s0 = send("xs0")
+    s1 = send("a0", [s0])
+    s1 = send("a1", [s1])
+    s1 = send("a2", [s1])
+
+    ts(C(6), C(1), 2.0, ALU.is_lt)
+    ts(C(7), C(1), 9.0, ALU.is_ge)
+    ts(C(8), C(1), 6.0, ALU.is_lt)
+    ts(C(9), C(1), 6.0, ALU.is_ge)
+    ts(a("col", 39, 42), a("inn", 0, 3), C(9), ALU.mult)
+    for t in range(R):
+        act(a("kC", 256 * t, 256 * t + 256), a("K0f", t, 1024, 4), bias=C(39 + t), scale=C(8))
+    sq = a("inp", 16, 144)
+    ts(a("P1a"), sq, 2.0, ALU.is_equal, C(6), ALU.mult)
+    ts(a("P1b"), sq, 1.0, ALU.is_equal, M(7), ALU.mult)
+    ts(a("P2a"), sq, 4.0, ALU.is_equal, C(6), ALU.mult)
+    act(a("P2b"), a("Id"), scale=C(7))
+    tt(a("P2a"), a("P2a"), a("P2b"), ALU.add)
+    ts(a("Pm1"), sq, 1.0, ALU.is_equal, M(0), ALU.mult)
+    ts(a("Pm6"), sq, 6.0, ALU.is_equal, M(0), ALU.mult)
+    act(a("hPm6"), a("Pm6"), scale=0.5)
+    act(a("hId"), a("Id"), scale=0.5)
+    act(a("M05"), a("Id"), scale=C(8))
+    act(a("Big6"), a("Big"), scale=M(6))
+    act(a("Big7"), a("Big"), scale=M(7))
+    ts(a("BO"), a("ing"), C(2), ALU.is_equal)
+    act(a("BOo"), a("BO"), scale=65536.0)
+    iota(a("Zm"), [[0, 128]], 0, 0)
+    act(a("o16"), a("Id"), bias=0.0625, scale=0.0)
+    act(a("mh"), a("kcon"), bias=-0.5, scale=0.0)
+    iota(a("one"), [[0, 320]], 1, 0)
+    iota(a("wed", 256, 320), [[0, 64]], 0, 0)
+    ts(a("lP15"), a("inn", 0, 16), 0.0, ALU.mult, C(1), ALU.add)
+    copy(a("lCol"), a("inn", 0, 16))
+    copy(a("diag"), ind(a("mask"), a("lP15")))
+    mset(a("tl", 0, 16), 0.5)
+    mset(a("tl", 16, 32), 0.0)
+    scan(a("pw", 0, 16), a("tl", 0, 16), a("tl", 16, 32), 131072.0, ALU.mult, ALU.add)
+    copy(a("thrB"), ind(a("pw", 0, 16), a("lP15")))
+    ts(a("tl", 16, 32), a("mask"), 0.5, ALU.mult)
+    tt(a("pw", 16, 32), a("pw", 0, 16), a("tl", 16, 32), ALU.mult)
+    red(C(14), a("pw", 16, 32))
+    act(a("BOd"), a("BO"), scale=C(14))
+    iota(a("iB"), [[1, 256]], 0, 0)
+    act(a("c3"), a("KC", 0, 256), scale=C(9))
+    iota(a("tl", 32, 48), [[64, 16]], 0, 0)
+    ts(C(15), C(1), 4.0, ALU.mult)
+    for t in range(R):
+        ts(a("vT", 16 * t, 16 * t + 16), a("tl", 32, 48), C(15), ALU.add, float(t), ALU.add)
+        iota(a("D%d" % t, 256, 320), [[0, 64]], 0, 0)
+        iota(a("xvS", 320 * t + 256, 320 * t + 320), [[0, 64]], 0, 0)
+        act(a("xvS", 320 * t, 320 * t + 256), a("X", t, 1024, 4))
+    iota(a("rs"), [[256, 4], [1, 16]], 0, 0)
+    ts(a("pos"), a("rs"), C(10), ALU.add)
+    iota(a("seg"), [[0, 4], [1, 16]], 0, 0)
+    ts(a("seg"), a("seg"), 0.0, ALU.is_equal, 8388608.0, ALU.mult)
+    ts(a("scol", 0, 4), a("inn", 0, 64, 16), C(1), ALU.add, -0.5, ALU.add)
+    tt(C(16), M(6), M(7), ALU.add)
+    ts(C(17), C(16), -1.0, ALU.mult, 1.0, ALU.add)
+    ts(C(18), M(6), 4.0, ALU.mult, M(7), ALU.add)
+    ts(C(19), M(0), 4.0, ALU.mult, C(16), ALU.add)
+    ts(C(20), M(6), -1.0, ALU.mult, 1.0, ALU.add)
+    t3 = a("inn", 0, 3)
+    ts(C(42), M(7), float(L), ALU.mult, M(6), ALU.add)
+    ts(C(43), M(7), float(B), ALU.mult)
+    ts(a("col", 24, 27), t3, C(42), ALU.mult, C(43), ALU.add)
+    ts(C(44), C(16), float(L), ALU.mult, M(0), ALU.add)
+    ts(C(45), C(16), float(B), ALU.mult)
+    ts(a("col", 27, 30), t3, C(44), ALU.mult, C(45), ALU.add)
+    ts(a("col", 46, 49), t3, float(L), ALU.mult, float(B), ALU.add)
+    ts(a("col", 30, 33), a("col", 46, 49), C(20), ALU.mult)
+    ts(a("col", 33, 36), a("mask", 9, 12), C(16), ALU.subtract, -1000.0, ALU.mult)
+    ts(C(49), C(16), -499.0, ALU.mult, -1.0, ALU.add)
+    ts(a("col", 36, 39), a("mask", 9, 12), 64.5, ALU.mult, C(49), ALU.add)
+    for t in range(R):
+        act(a("DD", 256 * t, 256 * t + 128), a("Id"), scale=C(33 + t))
+        act(a("DD", 256 * t + 128, 256 * t + 256), a("nId"), scale=M(9 + t))
+    s8 = {"ap": T.s8[0:8, :], "r": [("s8", 0, 128)], "n": 128, "sz": 4, "ps": False}
+    op("G", lambda q: q.iota(s8["ap"], [[1, 8], [0, 16]], 0, -1, allow_small_or_imprecise_dtypes=True), [], [s8], 0.4)
+    ts(s8, s8, 0.0, ALU.is_equal, 16.0, ALU.mult)
+    thi = {"ap": T.th32[0:8, 0:3], "r": [("th32", 0, 3)], "n": 3, "sz": 4, "ps": False}
+    thf = {"ap": T.thf[0:8, 0:3], "r": [("thf", 0, 3)], "n": 3, "sz": 4, "ps": False}
+    copy(thf, thi)
+    mm([(a("P7", 64, 67), s8, thf)])
+    copy(a("col", 21, 24), a("P7", 64, 67))
+
+    def scores(t, k0, k1, dyn, banks, kdst, cdst):
+        bd0, bd1, bc, bk = banks
+        n = k1 - k0
+        P = B + L * t if dyn else B
+        base = 4096 * (t & 1)
+        o1 = 256 * t
+        onA = A_ON_SCALAR.get((t, k0))
+        for k in range(k0, k1):
+            off = a("off1", o1 + 16 * k, o1 + 16 * k + 16)
+            mk = M((k + t) & 15)
+            if onA is not None:
+                act(a("Gf", onA + 256 * (k - k0), onA + 256 * (k - k0 + 1)), ind(a("K0f"), off), scale=mk)
+            else:
+                win = a("Kf", 0, P) if dyn and t else a("kin32")
+                ts(a("G", base + 256 * k, base + 256 * k + 256), ind(win, off), mk, ALU.mult)
+        if onA is not None:
+            mm([(a(bc, 0, 16 * n), big("Bigf", a_), a("Gf", onA + a_, onA + 256 * n, 16)) for a_ in range(16)])
+        else:
+            mm([(a(bc, 0, 16 * n), big("Big", a_), a("G", base + 256 * k0 + a_, base + 256 * k1, 16)) for a_ in range(16)])
+        copy(a("off2", o1 + 16 * k0, o1 + 16 * k1), a(bc, 0, 16 * n))
+        act(cdst, a(bc, 0, 16 * n))
+        for k in range(k0, k1):
+            tt(a("Cq", base + 256 * k, base + 256 * k + 256), ind(a("KC", 0, P), a("off2", o1 + 16 * k, o1 + 16 * k + 16)),
+               a("kC", 256 * t, 256 * t + 256), ALU.is_equal)
+        xv = a("xvS", 320 * t, 320 * t + 256)
+        for j, k in enumerate(range(k0, k1, 2)):
+            ke = min(k + 2, k1)
+            bank = (bd0, bd1)[j & 1]
+            w_ = 256 * (ke - k)
+            xc = a("xc", base + 256 * k, base + 256 * ke)
+            act(xc, ind(a("X", 0, P), a("off2", o1 + 16 * k, o1 + 16 * ke)))
+            mm([(a(bank, 0, w_), a("Id"), xc)] + [(a(bank, 256 * u, 256 * u + 256), a("nId"), xv) for u in range(ke - k)])
+            act(a("ad", base + 256 * k, base + 256 * ke), a(bank, 0, w_), ACT.Abs, scale=16.0)
+        o = a(bk, 0, 16 * n)
+        mm([(o, a("Id"), a("kcon", 16 * k0, 16 * k1))]
+           + [(o, big("BigC", a_), a("Cq", base + 256 * k0 + a_, base + 256 * k1, 16)) for a_ in range(16)], True, False)
+        mm([(o, big("Big", a_), a("ad", base + 256 * k0 + a_, base + 256 * k1, 16)) for a_ in range(16)], False, True)
+        if dyn:
+            copy(kdst, o)
+        else:
+            act(kdst, o)
+
+    def tree(src, lo, n, tmp, dst, f):
+        cur, cl, at = src, lo, 0
+        while n > 1:
+            h = (n + 1) // 2
+            o = dst if h == 1 else a(tmp, at, at + 16 * h)
+            tt(o, a(cur, cl, cl + 16 * h), a(cur, cl + 16 * (n - h), cl + 16 * n), f)
+            cur, cl, at, n = tmp, at, at + 16 * h, h
+
+    def argmin(kn, cn_, lo, n, kdst, cps, t0, t1, t2):
+        tree(kn, lo, n, t0, kdst, ALU.min)
+        e = a(t1, 0, 16 * n)
+        tt(e, ind(kdst, a("lP15", 0, n)), a(kn, lo, lo + 16 * n), ALU.is_equal)
+        tt(a(t2, 0, 16 * n), e, a(cn_, lo, lo + 16 * n), ALU.mult)
+        mm([(cps, a("Id"), a(t2, 16 * j, 16 * j + 16)) for j in range(n)])
+
+    STAT = [[(0, 4), (4, 8), (8, 12)], [(0, 5), (9, 13), (13, 16)], [(0, 4), (9, 13), (13, 16)]]
+    DYN = [(12, 16), (5, 9), (4, 9)]
+    SB, DB = ("P0", "P1", "P2", "P3"), ("P4", "P5", "P6", "P7")
+
+    def static_part(t):
+        at = 192 * t
+        for (k0, k1) in STAT[t]:
+            n = 16 * (k1 - k0)
+            scores(t, k0, k1, False, SB, a("key1", at, at + n), a("c1", at, at + n))
+            at += n
+        argmin("key1", "c1", 192 * t, (at - 192 * t) // 16, a("key2", 96 * t, 96 * t + 16), a("P3", 0, 16), "ta", "tb", "tc")
+        act(a("c2", 96 * t, 96 * t + 16), a("P3", 0, 16))
+
+    def dynamic_part(t):
+        n0 = B + L * t
+        c0 = 24 + 8 * t
+        k0, k1 = DYN[t]
+        nd = k1 - k0
+        act(a("DS%d" % t), ind(a("Kf" if t else "K0f", 0, 1024), a("aR%d" % t)))
+        sd = send("d%d" % t)
+        if t == 0:
+            send("xs2", [sd])
+            send("xs1", [sd])
+            kv = a("kvs", 0, 256)
+            thr = C(21)
+        else:
+            kv = a("kvd", 256 * t, 256 * t + 256)
+            copy(kv, a("Kf", t, 1024, 4))
+            for j, nm in enumerate(("Big6", "Big7")):
+                mm([(a("P7", 16 * j, 16 * j + 16), big(nm, a_), a("kvd", 256 * t + a_, 256 * t + 256, 16)) for a_ in range(16)])
+            copy(a("off1", 256 * t + 96, 256 * t + 128), a("P7", 0, 32))
+            thr = a("thr", t, t + 1)
+        scores(t, k0, k1, True, DB, a("key2", 96 * t + 16, 96 * t + 16 + 16 * nd), a("c2", 96 * t + 16, 96 * t + 16 + 16 * nd))
+        argmin("key2", "c2", 96 * t, nd + 1, a("km"), a("P6", 0, 16), "td", "te", "tf")
+        ts(a("iv"), a("km"), BIGK, ALU.is_ge, -4096.0, ALU.mult)
+        ts(a("nc"), a("km"), thr, ALU.is_ge, 2047.0, ALU.mult)
+        tt(a("mT"), a("P6", 0, 16), a("nc"), ALU.max)
+        tt(a("mS"), a("P6", 0, 16), a("iv"), ALU.add)
+        tt(a("Em"), ind(a("mT"), a("lCol")), a("diag"), ALU.mult)
+        mm([(a("P6", 0, 256), a("BO"), a("Em"))])
+        copy(a("mB"), a("P6", 0, 256))
+        ts(a("En"), a("mB"), 2047.0, ALU.is_equal, 4096.0, ALU.mult)
+        mm([(a("P7", 0, 256), a("BO"), a("En"))], True, False)
+        for b_ in range(16):
+            lo = 272 * b_
+            ts(a("eq", lo, 256 * b_ + 256), a("mB", 16 * b_, 256), a("mS", b_, b_ + 1), ALU.is_equal)
+            lst = [(a("P7", 16 * b_, 16 * b_ + 16), a("BOd"), a("eq", lo, lo + 16))]
+            if b_ < 15:
+                lst.append((a("P7", 16 * b_ + 16, 256), a("BOo"), a("eq", lo + 16, 256 * b_ + 256)))
+            mm(lst, False, b_ == 15)
+        tt(a("dmv"), a("mS"), a("vT", 16 * t, 16 * t + 16), ALU.subtract)
+        ts(a("dmv"), a("dmv"), 0.0625, ALU.mult)
+        ts(a("cn"), a("iB"), C(20), ALU.mult, C(30 + t), ALU.add)
+        ts(a("cv2"), a("iB"), C(19), ALU.mult, C(27 + t), ALU.add)
+        act(a("cvn"), a("iB"), bias=C(24 + t), scale=C(18))
+        mm([(a("P4", 0, 256), a("Pm6"), a("mB")), (a("P4", 0, 256), a("Id"), a("cn")), (a("P4", 0, 256), a("nId"), kv)])
+        wed = a("wed", 0, 256)
+        tt(wed, a("P7", 0, 256), a("thrB"), ALU.is_lt)
+        mm([(a("P6", 0, 16), big("Big", a_), a("wed", a_, 256, 16)) for a_ in range(16)])
+        scan(a("cum"), a("one"), a("wed"), -1.0, ALU.add, ALU.subtract)
+        nv = 2 if t in COUNT_ON_V else 0
+        for c in range(nv):
+            ts(a("jv", 320 * c, 320 * c + 320), a("cum"), a("scol", c, c + 1), ALU.is_lt, 0.5, ALU.subtract)
+            red(a("acc", c, c + 1), a("jv", 320 * c, 320 * c + 320))
+        for c in range(nv, 4):
+            act(a("junk"), a("cum"), ACT.Sign, a("scol", c, c + 1), -1.0, a("acc", c, c + 1))
+        tt(a("t1"), a("P6", 0, 16), a("dmv"), ALU.mult)
+        tt(a("t2"), a("t1"), a("vT", 16 * t, 16 * t + 16), ALU.add)
+        copy(a("msl"), a("t2"))
+        if t in KM_ON_V:
+            ts(a("kmz"), ind(a("Kf", 0, n0), a("msl")), C(17), ALU.mult)
+        else:
+            act(a("kmz"), ind(a("Kf", 0, n0), a("msl")), scale=C(17))
+        mm([(a("P5", 0, 256), a("DD", 256 * t, 256 * t + 128), wed), (a("P5", 0, 256), a("DD", 256 * t + 128, 256 * t + 256), a("cum", 0, 256))])
+        act(a("Fv"), a("P5", 0, 256), ACT.Sign, C(36 + t))
+        tt(a("prV"), a("P4", 0, 256), a("Fv"), ALU.mult)
+        o = a("P7", 0, 256)
+        mm([(o, a("P1a"), kv), (o, a("P1b"), kv), (o, a("nId"), kv), (o, a("Pm1"), a("mB")), (o, a("Id"), a("cv2"))], True, False)
+        mm([(o, a("P2a"), a("kmz"))], False, True)
+        tt(ind(a("Kf", 0, n0), a("msl")), a("kmz"), a("cvn"), ALU.add)
+        mm([(a("P6", 0, 256), l_, r_) for l_, r_ in ((a("hPm6"), a("mB")), (a("hId"), a("cn")), (a("hId"), kv), (a("hId"), a("prV")))])
+        act(a("Kf", t, 1024, 4), a("P6", 0, 256))
+        tt(a("prC"), o, wed, ALU.mult)
+        mm([(o, a("Id"), a("prC")), (o, a("Id"), kv)])
+        if t < R - 1:
+            o2 = a("P7", 256, 512)
+            mm([(o2, a("M05"), a("prC")), (o2, a("M05"), kv), (o2, a("Id"), a("c3"))])
+        act(a("Kf", n0, n0 + L), o)
+        if t < R - 1:
+            act(a("KC", n0, n0 + L), o2)
+        if t == 1:
+            dma("S", T.yk[:, 0:n0 + L], T.Kf[:, 0:n0 + L], [a("Kf", 0, n0 + L)], [a("yk", 0, W)], 850e3)
+        if t == 2:
+            dma("S", T.yk[:, n0:W], T.Kf[:, n0:W], [a("Kf", n0, W)], [], 130e3)
+            for j, row in enumerate((6, 7, 11)):
+                dma("S", T.yk[row:128:16, 0:n0], T.Kf[row:128:16, 0:n0], [a("Kf", 0, n0), a("yk", 0, W)], [], 60e3)
+        act(a("sm"), ind(a("X", 0, n0), a("msl")))
+        mm([(a("P6", 256, 512), a("hId"), r_) for r_ in (a("xvS", 320 * t, 320 * t + 256), a("mh"), a("sm"))])
+        act(a("sy"), a("P6", 256, 512), bias=MAGIC)
+        act(a("X", n0, n0 + L), a("sy"), bias=-MAGIC)
+        if nv:
+            ts(a("lan", 0, nv), a("acc", 0, nv), 160.0, ALU.add)
+        ts(a("lan", nv, 4), a("acc", nv, 4), 0.5, ALU.mult, 160.0, ALU.add)
+        lan = a("lan", 0, 4)
+        copy(a("Dc"), ind(a("D%d" % t), lan))
+        act(a("xvc"), ind(a("xvS", 320 * t, 320 * t + 320), lan))
+        xqw = a("XQ%d" % t)
+        for h, bank in enumerate(("P5", "P4")):
+            mm([(a(bank), a("Zm"), a("X", 0, 512))]
+               + [(a(bank, k, 512, 16), a("nId"), a("xvc", 32 * h, 32 * h + 32)) for k in range(16)], True, False)
+            xq = a("xq", 512 * h, 512 * h + 512)
+            src = ind(xqw, a("Dc", 32 * h, 32 * h + 32))
+            if h == 0 or t in XQ_ON_A:
+                act(xq, src)
+            else:
+                copy(xq, src)
+            mm([(a(bank), a("Id"), xq)], False, True)
+            aq = {"ap": T.aq[:, 2 * h:2 * h + 2, :], "r": [("aq", 512 * h, 512 * h + 512)], "n": 512, "sz": 2, "ps": False}
+            act(aq, a(bank), ACT.Abs, scale=1024.0)
+        o = a("P6", 0, 64)
+        mm([(o, a("Id"), a("pos"))] + [(o, big("Big", a_), {"ap": T.aq[:, :, 16 * a_:16 * a_ + 16], "r": [("aq", 0, 1024)], "n": 64, "sz": 2, "ps": False})
+                                       for a_ in range(16)])
+        scan(a("rs"), a("seg"), o, 0.0, ALU.add, ALU.min)
+        copy(a("ri", 0, 4), a("rs", 15, 64, 16))
+        ts(a("rj", 0, 4), a("ri", 0, 4), 1023, ALU.bitwise_and)
+        copy(a("rl", 0, 4), a("rj", 0, 4))
+        copy(a("near"), ind(a("xq"), a("rl", 0, 4)))
+        copy(ind(a("X", n0, n0 + 320), lan), a("near"))
+        if t == 0:
+            send("xn02", [send("xn01")])
+        if t == 1:
+            send("xn12")
+        dma("S", T.yx[:, L * t:L * t + L], T.X[:, n0:n0 + L], [a("X", n0, n0 + L)], [], 65e3)
+        if t < R - 1:
+            mm([(a("P6", 0, 1), a("o16"), a("cum", 255, 256))])
+            ts(a("zi", 0, 1), a("P6", 0, 1), -1.0, ALU.mult, 2040.0, ALU.add)
+            ts(a("zi", 1, 2), a("zi", 0, 1), 15, ALU.bitwise_and)
+            ts(a("thr", t + 1, t + 2), a("zi", 1, 2), 16.0, ALU.mult, C(22 + t), ALU.add)
+
+    static_part(0)
+    dynamic_part(0)
+    for t in (1, 2):
+        first_lists(t, "P2")
+        static_part(t)
+        dynamic_part(t)
+
+    emit(ops, Q, T, sent[0])
+
+
+_S["yk"] = (W, F32)
+LOG = []
+PLAN = []
+ITER, NOISE = [2500], [0.5, 2.0, 4.0, 8.0, 14.0]
+SCALES = [{"l": 1.0}, {"l": 2.0, "P": 1.2, "X": 1.4}, {"l": 1.0, "V": 0.85, "A": 0.85, "X": 1.3}]
+
+
+def emit(ops, Q, T, sent):
+    n = len(ops)
+    succ = [[] for _ in ops]
+    for i, o in enumerate(ops):
+        for d in o["deps"]:
+            succ[d].append(i)
+
+    def lag(d, i):
+        if ops[d]["e"] == ops[i]["e"]:
+            return 0.0 if ops[d]["e"] == "P" else 0.06
+        return 0.12
+
+    def hold(i):
+        o = ops[i]
+        return 0.0 if o["e"] == "X" else (0.1 if o["kind"] == "d" else o["cost"])
+
+    def place(seq, pre, back):
+        st = [0.0] * n
+        busy = {e: [] for e in "VAPGSX"}
+        for i in seq:
+            c, h = ops[i]["cost"], hold(i)
+            t = 0.0
+            for d in pre[i]:
+                x = st[d] + ops[d]["cost"] + lag(d, i)
+                if x > t:
+                    t = x
+            off = c - h if back else 0.0
+            t += off
+            lst = busy[ops[i]["e"]]
+            k = len(lst)
+            while k > 0 and lst[k - 1][1] > t:
+                k -= 1
+            while k < len(lst) and lst[k][0] < t + h:
+                t = max(t, lst[k][1])
+                k += 1
+            if h:
+                lst.insert(k, (t, t + h))
+            st[i] = t - off
+        return st
+
+    def replay(order, scale):
+        fin = [0.0] * n
+        free = {e: 0.0 for e in "VAPGSX"}
+        for i in order:
+            o = ops[i]
+            t = free[o["e"]] if o["e"] != "X" else 0.0
+            for d in o["deps"]:
+                t = max(t, fin[d] + lag(d, i) * scale["l"])
+            f = scale.get(o["e"], 1.0)
+            fin[i] = t + o["cost"] * f
+            free[o["e"]] = t + hold(i) * f
+        return max(fin)
+
+    if not PLAN:
+        pre = [list(o["deps"]) for o in ops]
+        pr = [0.0] * n
+        for i in range(n - 1, -1, -1):
+            pr[i] = ops[i]["cost"] + max([pr[j] + lag(i, j) for j in succ[i]] or [0.0])
+        seq = sorted(range(n), key=lambda i: (-pr[i], i))
+        best, rnd = None, 12345
+        for it in range(ITER[0]):
+            st = place(seq, pre, False)
+            order = sorted(range(n), key=lambda i: (st[i], i))
+            val = sum(replay(order, sc) for sc in SCALES)
+            if best is None or val < best[0]:
+                best = (val, order, st)
+            base = st if it % 4 else best[2]
+            seq = sorted(range(n), key=lambda i: (-(base[i] + ops[i]["cost"]), -i))
+            bt = place(seq, succ, True)
+            key = [0.0] * n
+            for i in range(n):
+                rnd = (rnd * 1103515245 + 12345) % 2147483648
+                key[i] = -(bt[i] + ops[i]["cost"]) + (rnd / 2147483648.0) * NOISE[it // 4 % len(NOISE)] * (it % 4 == 0)
+            for i in range(n):
+                for d in pre[i]:
+                    key[i] = max(key[i], key[d] + 1e-6)
+            seq = sorted(range(n), key=lambda i: (key[i], i))
+        PLAN.append(best)
+    order = PLAN[0][1]
+    for i in range(n):
+        ops[i]["t"] = (PLAN[0][2][i], PLAN[0][2][i] + ops[i]["cost"])
+    cnt = {}
+    known = {e: {} for e in "VAPGS"}
+    nd = 0
+    total = {}
+    for i in order:
+        o = ops[i]
+        e = o["e"]
+        if e == "X":
+            o["done"] = {o["wait"][0]: o["wait"][1]}
+            o["tok"] = o["wait"]
+            total[o["wait"][0]] = o["wait"][1]
+            continue
+        kn = known[e]
+        need = {}
+        for d in o["deps"]:
+            od = ops[d]
+            if od["kind"] == "r" or (e == "P" and od["e"] == "P"):
+                continue
+            s, v = od["tok"]
+            if kn.get(s, 0) < v:
+                need[s] = max(need.get(s, 0), v)
+        for d in o["deps"]:
+            for s, v in ops[d].get("done", {}).items():
+                if ops[d]["kind"] != "r" and not (e == "P" and ops[d]["e"] == "P") and ops[d]["tok"][0] != s and need.get(s, 0) and need[s] <= v:
+                    need[s] = 0
+        for s, v in need.items():
+            if v:
+                Q[e].wait_ge(T.sem[s], v)
+        for d in o["deps"]:
+            od = ops[d]
+            if od["kind"] == "r" or (e == "P" and od["e"] == "P"):
+                continue
+            for s, v in od["done"].items():
+                kn[s] = max(kn.get(s, 0), v)
+        ins = o["fn"](Q[e])
+        if o["kind"] == "r":
+            continue
+        if o["kind"] == "d":
+            s, v = "m%d" % nd, 16
+            nd += 1
+            ins.then_inc(T.sem[s], 16)
+        else:
+            s = "s" + e
+            v = cnt[s] = cnt.get(s, 0) + 1
+            ins.then_inc(T.sem[s], 1)
+        o["tok"] = (s, v)
+        o["done"] = dict(kn)
+        o["done"][s] = v
+        total[s] = v
+    for s, v in total.items():
+        if max(known[e].get(s, 0) for e in known) < v:
+            Q["S"].wait_ge(T.sem[s], v)
+    Q["G"].wait_ge(T.sem.sent, sent)
+    LOG[:] = [ops, order]

@@ -1,5 +1,5 @@
-from concourse.bass import DstId, RemoteDMATransfer
-from concourse.mybir import dt, AluOpType, AxisListType, ActivationFunctionType
+import math
+from concourse.mybir import AluOpType, AxisListType, ActivationFunctionType
 
 ALU = AluOpType
 ACT = ActivationFunctionType
@@ -33,7 +33,9 @@ _S = {
 }
 _S.update({"tf": (96, F16), "tc": (192, F16), "kC": (768, F32), "jv": (640, BF), "DD": (768, BF), "hPm6": (128, BF), "hId": (128, BF), "mh": (256, BF),
            "o16": (128, BF), "cum": (320, BF), "sm": (256, BF)})
-del _S["Lm"], _S["xvm"]
+_S.update({"xvT": (128, BF), "Eg": (1024, BF), "oi": (48, I32), "Rs": (2048, BF), "mH": (16, F16)})
+for _n in ("Em", "diag", "Lm", "xvm", "Zm", "mh", "c3", "M05", "Big7"):
+    del _S[_n]
 POOL = {}
 for _p, _d, _names in (("poolf", F32, "km mT mS iv nc dmv t1 t2 acc thr scol td te pw tl vT seg rs"), ("pooli", I32, "aI aJ ri rj zi pI"),
                        ("poolu", U16, "lP15 lCol lPerm msl lan rl Dc")):
@@ -44,6 +46,7 @@ for _p, _d, _names in (("poolf", F32, "km mT mS iv nc dmv t1 t2 acc thr scol td 
     _S[_p] = (_at, _d)
 SCRATCH = {k: ("sbuf", [128, v[0]], v[1]) for k, v in _S.items() if k not in POOL}
 SCRATCH["aq"] = ("sbuf", [128, 4, 256], BF)
+SCRATCH["eq"] = ("sbuf", [128, 16, 256], BF)
 for _b in range(8):
     SCRATCH["P%d" % _b] = ("psum", [128, 512], F32)
 NDMA = 40
@@ -52,6 +55,8 @@ SEMAPHORES = ["sV", "sA", "sP", "sG", "sent"] + ["m%d" % i for i in range(NDMA)]
 SIZE = {F32: 4, BF: 2, F16: 2, I32: 4, U16: 2}
 A_ON_SCALAR = {(0, 12): 0, (0, 8): 1024, (1, 9): 0, (2, 9): 1024}
 COUNT_ON_V, KM_ON_V, XQ_ON_A = [2], [2], [0, 1]
+XC_ON_V = []
+LAT = [4.5, 50e3]
 CYC = 0.83e-3 * 1.25
 PEC = 0.42e-3 * 1.25
 
@@ -153,7 +158,9 @@ def rank_program(g, core, T, topo):
                 lst[:] = [e for e in lst if not (lo <= e[0] and e[1] <= hi)]
             lst.append((lo, hi, i, wr))
         deps.discard(i)
-        ops.append({"e": eng, "fn": fn, "deps": deps, "cost": cost, "kind": kind, "wait": wait})
+        typ = "x" if kind != "c" else "s" if any("win" in x for x in writes) else "g" if any("win" in x for x in reads) else "c"
+        cost *= PLANF.get(typ, 1.0)
+        ops.append({"e": eng, "typ": typ, "fn": fn, "deps": deps, "cost": cost, "kind": kind, "wait": wait})
         return i
 
     def vcost(ins, out, two=False):
@@ -202,11 +209,11 @@ def rank_program(g, core, T, topo):
         c = 0.065 + (i["n"] * 1.56 if "win" in i else max(64, i["n"])) * CYC
         return op("A", fn, [i] + cols(bias, scale), [o] + cols(accum), c)
 
-    def mm(lst, first=True, final=True):
+    def mm(lst, first=True, final=True, each=False):
         def fn(q):
             ins = None
             for j, (o, l_, r_) in enumerate(lst):
-                ins = q.matmul(o["ap"], l_["ap"], r_["ap"], first and j == 0, final and j == len(lst) - 1)
+                ins = q.matmul(o["ap"], l_["ap"], r_["ap"], each or (first and j == 0), each or (final and j == len(lst) - 1))
             return ins
         c = sum(max(64, r_["n"]) * (4 if r_["sz"] == 4 else 1) for o, l_, r_ in lst) * PEC
         return op("P", fn, [x for e in lst for x in e[1:]], [e[0] for e in lst], c)
@@ -223,6 +230,7 @@ def rank_program(g, core, T, topo):
 
     fl = flows(T)
     sent = [0]
+    ARR = {}
 
     def send(name, after=()):
         t, kind, (sn, sl, sh), (dn, dl, dh) = fl[name]
@@ -238,9 +246,16 @@ def rank_program(g, core, T, topo):
         frm = (rank - far) % N if kind == "ask" else (rank + far) % N
         d2, r2 = route(T, topo, frm, name)
         cnt = nbits(topo.mask(T.cores[frm] if r2 is None else r2, core))
-        lat = (3.5 + nb / 60e3) * (1 if rel is None else 2)
+        lat = (LAT[0] + nb / LAT[1]) * (1 if rel is None else 2)
+        ARR[name] = len(ops)
         op("X", None, [], [a(dn, dl, dh)], lat, "x", [s], (name, cnt))
         return s
+
+    def top64(nm, lo, hi):
+        return {"ap": T[nm][0:64, lo:hi], "r": [(nm, lo, hi)], "n": hi - lo, "sz": 2, "ps": False}
+
+    def eqp(b_, lo, hi):
+        return {"ap": T.eq[:, b_, lo:hi], "r": [("eq", 256 * b_ + lo, 256 * b_ + hi)], "n": hi - lo, "sz": 2, "ps": False}
 
     def C(j):
         return a("col", j, j + 1)
@@ -302,7 +317,6 @@ def rank_program(g, core, T, topo):
     kc_ops = [dma("S", T.KC[16 * g_:16 * g_ + 6, 0:B], T.K0f[16 * g_:16 * g_ + 6, :], [a("K0f"), a("KC", 0, B)], [], 60e3)
               for g_ in range(8)]
     last["KC"] = [(0, B, j, True) for j in kc_ops]
-    dma("S", T.Kf[:, 0:B], T.K0f[:, :], [a("K0f")], [a("Kf", 0, B)], 600e3, kc_ops)
 
     copy(a("col", 11, 14), a("w32", 0, 3))
     for t in range(R):
@@ -315,6 +329,7 @@ def rank_program(g, core, T, topo):
     s1 = send("a0", [s0])
     s1 = send("a1", [s1])
     s1 = send("a2", [s1])
+    dma("S", T.Kf[:, 0:B], T.K0f[:, :], [a("K0f")], [a("Kf", 0, B)], 600e3, [ARR["a0"]])
 
     ts(C(6), C(1), 2.0, ALU.is_lt)
     ts(C(7), C(1), 9.0, ALU.is_ge)
@@ -333,19 +348,20 @@ def rank_program(g, core, T, topo):
     ts(a("Pm6"), sq, 6.0, ALU.is_equal, M(0), ALU.mult)
     act(a("hPm6"), a("Pm6"), scale=0.5)
     act(a("hId"), a("Id"), scale=0.5)
-    act(a("M05"), a("Id"), scale=C(8))
-    act(a("Big6"), a("Big"), scale=M(6))
-    act(a("Big7"), a("Big"), scale=M(7))
+    ts(C(50), M(7), 2048.0, ALU.mult, M(6), ALU.add)
+    act(a("Big6"), a("Big"), scale=C(50))
+    tt(a("P1a"), a("P1a"), a("P1b"), ALU.add)
+    tt(a("P1a"), a("P1a"), a("nId"), ALU.add)
     ts(a("BO"), a("ing"), C(2), ALU.is_equal)
     act(a("BOo"), a("BO"), scale=65536.0)
-    iota(a("Zm"), [[0, 128]], 0, 0)
+    iota(top64("Eg", 0, 1024), [[1, 64], [0, 16]], 0, -1)
+    ts(top64("Eg", 0, 1024), top64("Eg", 0, 1024), 0.0, ALU.is_equal)
     act(a("o16"), a("Id"), bias=0.0625, scale=0.0)
-    act(a("mh"), a("kcon"), bias=-0.5, scale=0.0)
     iota(a("one"), [[0, 320]], 1, 0)
     iota(a("wed", 256, 320), [[0, 64]], 0, 0)
     ts(a("lP15"), a("inn", 0, 16), 0.0, ALU.mult, C(1), ALU.add)
-    copy(a("lCol"), a("inn", 0, 16))
-    copy(a("diag"), ind(a("mask"), a("lP15")))
+    for a_ in range(16):
+        act(a("Rs", 128 * a_, 128 * a_ + 128), a("BO"), scale=M(a_))
     mset(a("tl", 0, 16), 0.5)
     mset(a("tl", 16, 32), 0.0)
     scan(a("pw", 0, 16), a("tl", 0, 16), a("tl", 16, 32), 131072.0, ALU.mult, ALU.add)
@@ -355,7 +371,7 @@ def rank_program(g, core, T, topo):
     red(C(14), a("pw", 16, 32))
     act(a("BOd"), a("BO"), scale=C(14))
     iota(a("iB"), [[1, 256]], 0, 0)
-    act(a("c3"), a("KC", 0, 256), scale=C(9))
+    ts(a("col", 51, 55), a("inn", 0, 4), C(9), ALU.mult)
     iota(a("tl", 32, 48), [[64, 16]], 0, 0)
     ts(C(15), C(1), 4.0, ALU.mult)
     for t in range(R):
@@ -404,20 +420,29 @@ def rank_program(g, core, T, topo):
         base = 4096 * (t & 1)
         o1 = 256 * t
         onA = A_ON_SCALAR.get((t, k0))
-        for k in range(k0, k1):
-            off = a("off1", o1 + 16 * k, o1 + 16 * k + 16)
-            mk = M((k + t) & 15)
+        late = dyn and t > 0
+        ks = [k for k in range(k0, k1) if k not in (6, 7)] + [6, 7] if late else list(range(k0, k1))
+        if late:
+            bc = bk
+        for s0, s1 in ([(0, n - 2), (n - 2, n)] if late else [(0, n)]):
+            if late and s0:
+                late_lists(t)
+            for s_ in range(s0, s1):
+                k = ks[s_]
+                off = a("off1", o1 + 16 * k, o1 + 16 * k + 16)
+                mk = M((k + t) & 15)
+                if onA is not None:
+                    act(a("Gf", onA + 256 * s_, onA + 256 * s_ + 256), ind(a("K0f"), off), scale=mk)
+                else:
+                    win = a("Kf", 0, P) if late else a("kin32")
+                    ts(a("G", base + 256 * (k0 + s_), base + 256 * (k0 + s_ + 1)), ind(win, off), mk, ALU.mult)
+            o = a(bc, 0, 16 * (s1 - s0))
             if onA is not None:
-                act(a("Gf", onA + 256 * (k - k0), onA + 256 * (k - k0 + 1)), ind(a("K0f"), off), scale=mk)
+                mm([(o, big("Bigf", a_), a("Gf", onA + a_, onA + 256 * n, 16)) for a_ in range(16)])
             else:
-                win = a("Kf", 0, P) if dyn and t else a("kin32")
-                ts(a("G", base + 256 * k, base + 256 * k + 256), ind(win, off), mk, ALU.mult)
-        if onA is not None:
-            mm([(a(bc, 0, 16 * n), big("Bigf", a_), a("Gf", onA + a_, onA + 256 * n, 16)) for a_ in range(16)])
-        else:
-            mm([(a(bc, 0, 16 * n), big("Big", a_), a("G", base + 256 * k0 + a_, base + 256 * k1, 16)) for a_ in range(16)])
-        copy(a("off2", o1 + 16 * k0, o1 + 16 * k1), a(bc, 0, 16 * n))
-        act(cdst, a(bc, 0, 16 * n))
+                mm([(o, big("Big", a_), a("G", base + 256 * (k0 + s0) + a_, base + 256 * (k0 + s1), 16)) for a_ in range(16)])
+            copy(a("off2", o1 + 16 * (k0 + s0), o1 + 16 * (k0 + s1)), o)
+            act(a(cdst[0], cdst[1] + 16 * s0, cdst[1] + 16 * s1), o)
         for k in range(k0, k1):
             tt(a("Cq", base + 256 * k, base + 256 * k + 256), ind(a("KC", 0, P), a("off2", o1 + 16 * k, o1 + 16 * k + 16)),
                a("kC", 256 * t, 256 * t + 256), ALU.is_equal)
@@ -427,17 +452,25 @@ def rank_program(g, core, T, topo):
             bank = (bd0, bd1)[j & 1]
             w_ = 256 * (ke - k)
             xc = a("xc", base + 256 * k, base + 256 * ke)
-            act(xc, ind(a("X", 0, P), a("off2", o1 + 16 * k, o1 + 16 * ke)))
+            (copy if late and (t, j) in XC_ON_V else act)(xc, ind(a("X", 0, P), a("off2", o1 + 16 * k, o1 + 16 * ke)))
             mm([(a(bank, 0, w_), a("Id"), xc)] + [(a(bank, 256 * u, 256 * u + 256), a("nId"), xv) for u in range(ke - k)])
             act(a("ad", base + 256 * k, base + 256 * ke), a(bank, 0, w_), ACT.Abs, scale=16.0)
         o = a(bk, 0, 16 * n)
-        mm([(o, a("Id"), a("kcon", 16 * k0, 16 * k1))]
-           + [(o, big("BigC", a_), a("Cq", base + 256 * k0 + a_, base + 256 * k1, 16)) for a_ in range(16)], True, False)
+        runs = [(0, n - 3), (n - 3, n - 2), (n - 2, n)] if late else [(0, n)]
+        mm([(o, big("BigC", a_), a("Cq", base + 256 * k0 + a_, base + 256 * k1, 16)) for a_ in range(16)]
+           + [(a(bk, 16 * u, 16 * v), a("Id"), a("kcon", 16 * ks[u], 16 * (ks[u] + v - u))) for u, v in runs], True, False)
         mm([(o, big("Big", a_), a("ad", base + 256 * k0 + a_, base + 256 * k1, 16)) for a_ in range(16)], False, True)
         if dyn:
             copy(kdst, o)
         else:
             act(kdst, o)
+
+    def late_lists(t):
+        mm([(a("P7", 0, 16), big("Big6", a_), a("kvd", 256 * t + a_, 256 * t + 256, 16)) for a_ in range(16)])
+        copy(a("oi", 0, 16), a("P7", 0, 16))
+        ts(a("oi", 16, 32), a("oi", 0, 16), 2047, ALU.bitwise_and)
+        ts(a("oi", 32, 48), a("oi", 0, 16), 11, ALU.logical_shift_right)
+        copy(a("off1", 256 * t + 96, 256 * t + 128), a("oi", 16, 48))
 
     def tree(src, lo, n, tmp, dst, f):
         cur, cl, at = src, lo, 0
@@ -462,7 +495,7 @@ def rank_program(g, core, T, topo):
         at = 192 * t
         for (k0, k1) in STAT[t]:
             n = 16 * (k1 - k0)
-            scores(t, k0, k1, False, SB, a("key1", at, at + n), a("c1", at, at + n))
+            scores(t, k0, k1, False, SB, a("key1", at, at + n), ("c1", at))
             at += n
         argmin("key1", "c1", 192 * t, (at - 192 * t) // 16, a("key2", 96 * t, 96 * t + 16), a("P3", 0, 16), "ta", "tb", "tc")
         act(a("c2", 96 * t, 96 * t + 16), a("P3", 0, 16))
@@ -482,28 +515,22 @@ def rank_program(g, core, T, topo):
         else:
             kv = a("kvd", 256 * t, 256 * t + 256)
             copy(kv, a("Kf", t, 1024, 4))
-            for j, nm in enumerate(("Big6", "Big7")):
-                mm([(a("P7", 16 * j, 16 * j + 16), big(nm, a_), a("kvd", 256 * t + a_, 256 * t + 256, 16)) for a_ in range(16)])
-            copy(a("off1", 256 * t + 96, 256 * t + 128), a("P7", 0, 32))
             thr = a("thr", t, t + 1)
-        scores(t, k0, k1, True, DB, a("key2", 96 * t + 16, 96 * t + 16 + 16 * nd), a("c2", 96 * t + 16, 96 * t + 16 + 16 * nd))
+        scores(t, k0, k1, True, DB, a("key2", 96 * t + 16, 96 * t + 16 + 16 * nd), ("c2", 96 * t + 16))
         argmin("key2", "c2", 96 * t, nd + 1, a("km"), a("P6", 0, 16), "td", "te", "tf")
         ts(a("iv"), a("km"), BIGK, ALU.is_ge, -4096.0, ALU.mult)
         ts(a("nc"), a("km"), thr, ALU.is_ge, 2047.0, ALU.mult)
-        tt(a("mT"), a("P6", 0, 16), a("nc"), ALU.max)
+        tt(a("mH"), a("P6", 0, 16), a("nc"), ALU.max)
         tt(a("mS"), a("P6", 0, 16), a("iv"), ALU.add)
-        tt(a("Em"), ind(a("mT"), a("lCol")), a("diag"), ALU.mult)
-        mm([(a("P6", 0, 256), a("BO"), a("Em"))])
-        copy(a("mB"), a("P6", 0, 256))
+        mm([(a("P5", a_, 256, 16), a("Rs", 128 * a_, 128 * a_ + 128), a("mH")) for a_ in range(16)], each=True)
+        copy(a("mB"), a("P5", 0, 256))
         ts(a("En"), a("mB"), 2047.0, ALU.is_equal, 4096.0, ALU.mult)
         mm([(a("P7", 0, 256), a("BO"), a("En"))], True, False)
         for b_ in range(16):
-            lo = 272 * b_
-            ts(a("eq", lo, 256 * b_ + 256), a("mB", 16 * b_, 256), a("mS", b_, b_ + 1), ALU.is_equal)
-            lst = [(a("P7", 16 * b_, 16 * b_ + 16), a("BOd"), a("eq", lo, lo + 16))]
+            ts(eqp(b_, 0, 256 - 16 * b_), a("mB", 16 * b_, 256), a("mS", b_, b_ + 1), ALU.is_equal)
             if b_ < 15:
-                lst.append((a("P7", 16 * b_ + 16, 256), a("BOo"), a("eq", lo + 16, 256 * b_ + 256)))
-            mm(lst, False, b_ == 15)
+                mm([(a("P7", 16 * b_ + 16, 256), a("BOo"), eqp(b_, 16, 256 - 16 * b_))], False, False)
+        mm([(a("P7", 0, 256), a("BOd"), {"ap": T.eq[:, :, 0:16], "r": [("eq", 0, 4096)], "n": 256, "sz": 2, "ps": False})], False, True)
         tt(a("dmv"), a("mS"), a("vT", 16 * t, 16 * t + 16), ALU.subtract)
         ts(a("dmv"), a("dmv"), 0.0625, ALU.mult)
         ts(a("cn"), a("iB"), C(20), ALU.mult, C(30 + t), ALU.add)
@@ -531,28 +558,27 @@ def rank_program(g, core, T, topo):
         act(a("Fv"), a("P5", 0, 256), ACT.Sign, C(36 + t))
         tt(a("prV"), a("P4", 0, 256), a("Fv"), ALU.mult)
         o = a("P7", 0, 256)
-        mm([(o, a("P1a"), kv), (o, a("P1b"), kv), (o, a("nId"), kv), (o, a("Pm1"), a("mB")), (o, a("Id"), a("cv2"))], True, False)
+        mm([(o, a("P1a"), kv), (o, a("Pm1"), a("mB")), (o, a("Id"), a("cv2"))], True, False)
         mm([(o, a("P2a"), a("kmz"))], False, True)
         tt(ind(a("Kf", 0, n0), a("msl")), a("kmz"), a("cvn"), ALU.add)
         mm([(a("P6", 0, 256), l_, r_) for l_, r_ in ((a("hPm6"), a("mB")), (a("hId"), a("cn")), (a("hId"), kv), (a("hId"), a("prV")))])
         act(a("Kf", t, 1024, 4), a("P6", 0, 256))
         tt(a("prC"), o, wed, ALU.mult)
         mm([(o, a("Id"), a("prC")), (o, a("Id"), kv)])
-        if t < R - 1:
-            o2 = a("P7", 256, 512)
-            mm([(o2, a("M05"), a("prC")), (o2, a("M05"), kv), (o2, a("Id"), a("c3"))])
         act(a("Kf", n0, n0 + L), o)
         if t < R - 1:
-            act(a("KC", n0, n0 + L), o2)
-        if t == 1:
-            dma("S", T.yk[:, 0:n0 + L], T.Kf[:, 0:n0 + L], [a("Kf", 0, n0 + L)], [a("yk", 0, W)], 850e3)
-        if t == 2:
-            dma("S", T.yk[:, n0:W], T.Kf[:, n0:W], [a("Kf", n0, W)], [], 130e3)
-            for j, row in enumerate((6, 7, 11)):
-                dma("S", T.yk[row:128:16, 0:n0], T.Kf[row:128:16, 0:n0], [a("Kf", 0, n0), a("yk", 0, W)], [], 60e3)
+            for r_ in range(4):
+                act(a("KC", n0 + r_, n0 + L, 4), a("Kf", n0 + r_, n0 + L, 4), bias=C(51 + r_), scale=C(8))
+        if t == 0:
+            dma("S", T.yk[:, 0:B], T.K0f[:, :], [a("K0f")], [a("yk", 0, B)], 600e3, [ARR["xs2"], ARR["xs1"]])
+        dma("S", T.yk[:, n0:n0 + L], T.Kf[:, n0:n0 + L], [a("Kf", n0, n0 + L)], [a("yk", n0, n0 + L)], 130e3)
+        if t:
+            for row in ((9, 10), (6, 7, 11))[t - 1]:
+                hi = n0 if row < 9 else 1024
+                dma("S", T.yk[row:128:16, 0:hi], T.Kf[row:128:16, 0:hi], [a("Kf", 0, hi), a("yk", 0, hi)], [], 60e3)
         act(a("sm"), ind(a("X", 0, n0), a("msl")))
-        mm([(a("P6", 256, 512), a("hId"), r_) for r_ in (a("xvS", 320 * t, 320 * t + 256), a("mh"), a("sm"))])
-        act(a("sy"), a("P6", 256, 512), bias=MAGIC)
+        mm([(a("P6", 256, 512), a("Id"), r_) for r_ in (a("xvS", 320 * t, 320 * t + 256), a("sm"))])
+        act(a("sy"), a("P6", 256, 512), bias=MAGIC, scale=0.4995)
         act(a("X", n0, n0 + L), a("sy"), bias=-MAGIC)
         if nv:
             ts(a("lan", 0, nv), a("acc", 0, nv), 160.0, ALU.add)
@@ -561,9 +587,11 @@ def rank_program(g, core, T, topo):
         copy(a("Dc"), ind(a("D%d" % t), lan))
         act(a("xvc"), ind(a("xvS", 320 * t, 320 * t + 320), lan))
         xqw = a("XQ%d" % t)
+        pt = {"ap": T.P5[0:64, 0:128], "r": [("P5", 0, 512)], "n": 128, "sz": 4, "ps": True}
+        mm([(pt, a("xvc"), a("nId"))])
+        act(top64("xvT", 0, 128), pt)
         for h, bank in enumerate(("P5", "P4")):
-            mm([(a(bank), a("Zm"), a("X", 0, 512))]
-               + [(a(bank, k, 512, 16), a("nId"), a("xvc", 32 * h, 32 * h + 32)) for k in range(16)], True, False)
+            mm([(a(bank), top64("xvT", 0, 128), top64("Eg", 512 * h, 512 * h + 512))], True, False)
             xq = a("xq", 512 * h, 512 * h + 512)
             src = ind(xqw, a("Dc", 32 * h, 32 * h + 32))
             if h == 0 or t in XQ_ON_A:
@@ -606,8 +634,11 @@ def rank_program(g, core, T, topo):
 _S["yk"] = (W, F32)
 LOG = []
 PLAN = []
-ITER, NOISE = [2500], [0.5, 2.0, 4.0, 8.0, 14.0]
-SCALES = [{"l": 1.0}, {"l": 2.0, "P": 1.2, "X": 1.4}, {"l": 1.0, "V": 0.85, "A": 0.85, "X": 1.3}]
+ITER, NOISE = [3000], [0.5, 2.0, 4.0, 8.0, 14.0]
+PLANF = {"c": 0.9, "g": 0.85, "s": 0.9}
+LAG = [0.3, 0.12]
+SCALES = [{"l": 0.55, "c": 0.82, "g": 0.62, "s": 0.6, "x": 0.8}, {"l": 0.7, "c": 0.85, "g": 0.82, "s": 0.85, "x": 0.9},
+          {"l": 0.55, "c": 1.0, "g": 1.0, "s": 1.0, "x": 1.0}, {"l": 0.55, "c": 1.16, "g": 1.45, "s": 1.6, "x": 1.0}]
 
 
 def emit(ops, Q, T, sent):
@@ -619,8 +650,8 @@ def emit(ops, Q, T, sent):
 
     def lag(d, i):
         if ops[d]["e"] == ops[i]["e"]:
-            return 0.0 if ops[d]["e"] == "P" else 0.06
-        return 0.12
+            return 0.0 if ops[d]["e"] == "P" else LAG[1]
+        return LAG[0]
 
     def hold(i):
         o = ops[i]
@@ -658,7 +689,7 @@ def emit(ops, Q, T, sent):
             t = free[o["e"]] if o["e"] != "X" else 0.0
             for d in o["deps"]:
                 t = max(t, fin[d] + lag(d, i) * scale["l"])
-            f = scale.get(o["e"], 1.0)
+            f = scale[o["typ"]] / PLANF.get(o["typ"], 1.0)
             fin[i] = t + o["cost"] * f
             free[o["e"]] = t + hold(i) * f
         return max(fin)
@@ -673,9 +704,10 @@ def emit(ops, Q, T, sent):
         for it in range(ITER[0]):
             st = place(seq, pre, False)
             order = sorted(range(n), key=lambda i: (st[i], i))
-            val = sum(replay(order, sc) for sc in SCALES)
+            vals = [replay(order, sc) for sc in SCALES]
+            val = sum(math.log(v) for v in vals)
             if best is None or val < best[0]:
-                best = (val, order, st)
+                best = (val, order, st, vals)
             base = st if it % 4 else best[2]
             seq = sorted(range(n), key=lambda i: (-(base[i] + ops[i]["cost"]), -i))
             bt = place(seq, succ, True)
@@ -688,7 +720,7 @@ def emit(ops, Q, T, sent):
                     key[i] = max(key[i], key[d] + 1e-6)
             seq = sorted(range(n), key=lambda i: (key[i], i))
         PLAN.append(best)
-    order = PLAN[0][1]
+    order = list(range(5)) + [i for i in PLAN[0][1] if i >= 5]
     for i in range(n):
         ops[i]["t"] = (PLAN[0][2][i], PLAN[0][2][i] + ops[i]["cost"])
     cnt = {}

@@ -4,7 +4,8 @@ from concourse.mybir import AluOpType, AxisListType, ActivationFunctionType
 ALU = AluOpType
 ACT = ActivationFunctionType
 N, B, L, R, W = 4, 1152, 256, 3, 1920
-BIGK = 131072.0
+BIGK = 4194304.0
+NONE = 2097152.0 + 256.0
 MAGIC = 12582912.0
 
 F32, BF, F16, I32, U16 = "float32", "bfloat16", "float16", "int32", "uint16"
@@ -14,31 +15,24 @@ _S = {
     "D0": (320, F32), "D1": (320, F32), "D2": (320, F32), "DS0": (L, F32), "DS1": (L, F32), "DS2": (L, F32),
     "aS": (48, U16), "aR0": (16, U16), "aR1": (16, U16), "aR2": (16, U16), "aI": (48, I32), "aJ": (48, I32),
     "w32": (4, I32), "th32": (4, I32), "thf": (4, F32),
-    "inp": (160, F32), "inn": (320, F32), "ing": (128, F32), "pI": (8, I32), "col": (64, F32), "mask": (16, F32),
-    "E0": (160, BF), "E1": (160, BF), "Id": (128, BF), "nId": (128, BF), "Zm": (128, BF), "Big": (144, BF), "Bigf": (144, F32),
-    "BigC": (144, BF), "Big6": (144, BF), "Big7": (144, BF), "BigW": (432, BF), "BO": (128, BF), "BOd": (128, BF), "BOo": (128, BF),
-    "P1a": (128, BF), "P1b": (128, BF), "P2a": (128, F32), "P2b": (128, F32), "Pm1": (128, BF), "Pm6": (128, BF), "M05": (128, BF),
-    "o16": (128, F32), "s8": (128, F32), "lP15": (16, U16), "lCol": (16, U16), "lPerm": (16, U16), "tl": (48, F32),
-    "diag": (256, BF), "kcon": (256, BF), "pw": (32, F32), "thrB": (256, F32), "iB": (256, BF), "c3": (256, BF), "one": (320, BF),
-    "pos": (64, F16), "seg": (64, F32), "vT": (48, F32), "scol": (8, F32), "junk": (320, BF),
-    "kvs": (768, F16), "kvd": (768, F16), "tr": (768, F32), "off1": (768, U16), "off2": (768, U16), "xvS": (960, BF), "xvm": (256, F32),
-    "G": (8192, F16), "Gf": (2048, F32), "Cq": (8192, BF), "xc": (8192, BF), "ad": (8192, BF),
-    "key1": (576, F32), "c1": (576, F32), "key2": (288, F32), "c2": (288, F32), "ta": (256, F32), "tb": (256, F32), "tc": (192, F32),
-    "td": (96, F32), "te": (96, F32), "km": (16, F32), "mT": (16, F32), "mS": (16, F32), "iv": (16, F32), "nc": (16, F32), "dmv": (16, F32),
-    "Em": (256, F16), "En": (256, BF), "mB": (256, F16), "eq": (4096, BF), "wed": (320, BF), "cum": (320, F32), "Lm": (256, F32), "Fv": (256, BF),
-    "t1": (16, F32), "t2": (16, F32), "msl": (16, U16), "kmz": (256, F32), "cvn": (256, F32), "cv2": (256, F16), "cn": (256, F16),
-    "prC": (256, F16), "prV": (256, F16), "sm": (256, F32), "sy": (256, F32), "acc": (8, F32), "lan": (8, U16), "Dc": (64, U16),
-    "xvc": (64, BF), "xq": (1024, BF), "rs": (64, F32), "ri": (8, I32), "rj": (8, I32), "rl": (8, U16), "near": (64, BF),
-    "zi": (8, I32), "thr": (8, F32),
+    "inp": (160, BF), "inn": (144, F32), "ing": (128, BF), "pI": (8, I32), "col": (64, F32), "mask": (16, F32),
+    "E0": (160, BF), "E1": (160, BF), "Id": (128, BF), "nId": (128, BF), "hId": (128, BF), "Big": (144, BF), "BigC": (144, BF),
+    "BigN": (144, BF), "BigW": (432, BF), "BO": (128, BF), "BOd": (128, BF), "BOo": (128, BF),
+    "mat": (1152, BF), "A3": (256, F32), "o16": (128, BF), "s8": (128, F32), "lP15": (16, U16), "lPerm": (16, U16), "tl": (48, F32),
+    "pw": (32, F32), "thrB": (256, F32), "iB": (256, BF), "one": (512, BF), "jm": (256, BF), "diag": (256, BF), "segm": (256, BF),
+    "pos": (64, F16), "seg": (64, F32), "nL": (48, F16), "nI": (48, F32), "scol": (8, F32), "junk": (320, BF), "jv": (640, BF),
+    "Rs": (2048, BF), "Eg": (1024, BF), "cv": (768, F16), "cvn": (768, F32),
+    "kvs": (768, F16), "kvd": (768, F16), "tr": (768, F32), "off1": (768, U16), "off2": (768, U16), "xv4": (3072, BF), "kC4": (3072, F16),
+    "G": (8192, F16), "Cq": (8192, BF), "xc": (8192, BF), "ad": (8192, BF), "cW": (816, F32), "best": (192, F32), "td": (64, F32),
+    "km": (16, I32), "wi": (16, I32), "wl": (16, U16), "nc": (16, BF), "Em": (256, F16), "mS": (256, F32), "mB": (256, F16),
+    "wed": (320, BF), "cum": (320, BF), "Fv": (256, BF), "ms": (16, F32), "msl": (16, U16), "kmz": (256, F32), "Pr": (256, F16),
+    "sm": (256, F16), "acc": (8, F32), "lan": (8, U16), "Dc": (64, U16), "xvc": (64, BF), "xvT": (128, BF), "xq": (1024, BF),
+    "rs": (64, F32), "ri": (8, I32), "rj": (8, I32), "rl": (8, U16), "near": (64, BF), "zi": (8, I32), "thr": (8, F32),
+    "eq": (4096, BF), "aq": (1024, BF), "kv2": (512, F16),
 }
-_S.update({"tf": (96, F16), "tc": (192, F16), "kC": (768, F32), "jv": (640, BF), "DD": (768, BF), "hPm6": (128, BF), "hId": (128, BF), "mh": (256, BF),
-           "o16": (128, BF), "cum": (320, BF), "sm": (256, BF)})
-_S.update({"xvT": (128, BF), "Eg": (1024, BF), "oi": (48, I32), "Rs": (2048, BF), "mH": (16, F16)})
-for _n in ("Em", "diag", "Lm", "xvm", "Zm", "mh", "c3", "M05", "Big7"):
-    del _S[_n]
 POOL = {}
-for _p, _d, _names in (("poolf", F32, "km mT mS iv nc dmv t1 t2 acc thr scol td te pw tl vT seg rs"), ("pooli", I32, "aI aJ ri rj zi pI"),
-                       ("poolu", U16, "lP15 lCol lPerm msl lan rl Dc")):
+for _p, _d, _names in (("poolf", F32, "ms acc thr scol td pw tl nI seg rs best"), ("pooli", I32, "aI aJ ri rj zi pI km wi"),
+                       ("poolu", U16, "lP15 lPerm msl lan rl Dc wl")):
     _at = 0
     for _n in _names.split():
         POOL[_n] = (_p, _at)
@@ -47,18 +41,25 @@ for _p, _d, _names in (("poolf", F32, "km mT mS iv nc dmv t1 t2 acc thr scol td 
 SCRATCH = {k: ("sbuf", [128, v[0]], v[1]) for k, v in _S.items() if k not in POOL}
 SCRATCH["aq"] = ("sbuf", [128, 4, 256], BF)
 SCRATCH["eq"] = ("sbuf", [128, 16, 256], BF)
+SCRATCH["kv2"] = ("sbuf", [128, 2, 256], F16)
 for _b in range(8):
     SCRATCH["P%d" % _b] = ("psum", [128, 512], F32)
-NDMA = 40
+_S["yk"] = (W, F32)
+NDMA = 80
 FLOWS = ["xs0", "xs1", "xs2", "a0", "a1", "a2", "d0", "d1", "d2", "xn01", "xn02", "xn12"]
 SEMAPHORES = ["sV", "sA", "sP", "sG", "sent"] + ["m%d" % i for i in range(NDMA)] + FLOWS + ["h" + f for f in FLOWS]
 SIZE = {F32: 4, BF: 2, F16: 2, I32: 4, U16: 2}
-A_ON_SCALAR = {(0, 12): 0, (0, 8): 1024, (1, 9): 0, (2, 9): 1024}
-COUNT_ON_V, KM_ON_V, XQ_ON_A = [2], [2], [0, 1]
-XC_ON_V = []
-LAT = [4.5, 50e3]
+LAT = [3.5, 50e3]
 CYC = 0.83e-3 * 1.25
 PEC = 0.42e-3 * 1.25
+
+BLOCKS = [
+    [([0, 1, 2, 3], "VAVA", "aa", 1), ([4, 5, 6, 7], "VAVA", "bb", 1), ([8, 9, 10, 11], "AAAA", "aa", 4), ([12, 13, 14, 15], "AAAA", "ab", 4)],
+    [([0, 1, 2, 3], "AAAA", "aa", 4), ([4, 9, 10, 11], "AAAA", "bb", 4), ([12, 13, 14, 15], "AAAA", "aa", 4), ([5, 8, 6, 7], "AAVA", "ab", 4)],
+    [([0, 1, 2, 3], "AAAA", "aa", 4), ([9, 10, 11, 12], "AAAA", "aa", 4), ([13, 14, 15], "AAA", "bb", 4), ([4, 5, 8, 6, 7], "AAAVA", "aab", 4)],
+]
+CFG = {"mB": "AAA", "count": [0, 0, 2], "km": "AAA", "xq": ["AA", "AA", "AV"], "sm": "AAA", "mS": "VVV", "ncol": "VVV", "F": "VVV",
+       "DS": "AAA", "kv2": "VA", "c": "A", "stride": True}
 
 
 def flows(T):
@@ -82,7 +83,6 @@ def route(T, topo, r, name):
     can = [c for c in topo.cores_of(src) if c != src and T.rank_of(c) is None and topo.may_write(c, dst)]
     same = [c for c in can if topo.die(c) == topo.die(src)]
     other = [c for c in can if topo.die(c) != topo.die(src)]
-    can = same + other
     if name.startswith("xs"):
         return dst, (same[0] if t == 0 else other[0])
     return dst, same[-1]
@@ -113,6 +113,21 @@ def relay_program(g, core, T, topo):
         g.wait_ge(T.sem.sent, sent)
 
 
+def meet(x, y):
+    if x[0] >= y[1] or y[0] >= x[1]:
+        return False
+    return not (CFG["stride"] and x[2] == y[2] > 1 and (x[0] - y[0]) % x[2])
+
+
+def runs(ks):
+    out, u = [], 0
+    for v in range(1, len(ks) + 1):
+        if v == len(ks) or ks[v] != ks[v - 1] + 1:
+            out.append((u, v))
+            u = v
+    return out
+
+
 def rank_program(g, core, T, topo):
     rank = T.rank_of(core)
     if rank is None:
@@ -122,15 +137,19 @@ def rank_program(g, core, T, topo):
     Q = {"V": g.vector, "A": g.scalar, "P": g.tensor, "G": g, "S": g.sync}
 
     def a(nm, lo=0, hi=None, st=1):
+        psum = nm[0] == "P" and nm[1:].isdigit()
         if hi is None:
-            hi = 512 if nm[0] == "P" and nm[1:].isdigit() else _S[nm][0]
+            hi = 512 if psum else _S[nm][0]
         if nm in POOL:
             nm, lo, hi = POOL[nm][0], lo + POOL[nm][1], hi + POOL[nm][1]
         ap = T[nm][:, lo:hi] if st == 1 else T[nm][:, lo:hi:st]
         n = len(range(lo, hi, st))
-        if nm[0] == "P" and nm[1:].isdigit():
-            return {"ap": ap, "r": [(nm, 0, 512)], "n": n, "sz": 4, "ps": True}
-        return {"ap": ap, "r": [(nm, lo, lo + (n - 1) * st + 1)], "n": n, "sz": SIZE[_S[nm][1]], "ps": False}
+        if psum:
+            return {"ap": ap, "r": [(nm, (0, 512, 1))], "n": n, "sz": 4, "ps": True}
+        return {"ap": ap, "r": [(nm, (lo, lo + (n - 1) * st + 1, st))], "n": n, "sz": SIZE[_S[nm][1]], "ps": False}
+
+    def view(ap, nm, lo, hi, n):
+        return {"ap": ap, "r": [(nm, (lo, hi, 1))], "n": n, "sz": SIZE[_S[nm][1]], "ps": False}
 
     def ind(win, off):
         return {"ap": win["ap"].indirect(off["ap"]), "r": win["r"] + off["r"], "n": 16 * off["n"], "sz": win["sz"], "ps": False,
@@ -148,15 +167,15 @@ def rank_program(g, core, T, topo):
                 acc += [(r_, True) for r_ in x["win"]] + [(r_, False) for r_ in x["off"]]
             else:
                 acc += [(r_, True) for r_ in x["r"]]
-        for (nm, lo, hi), wr in acc:
-            for (l2, h2, j, w2) in last.get(nm, []):
-                if l2 < hi and lo < h2 and (wr or w2):
+        for (nm, cs), wr in acc:
+            for (c2, j, w2) in last.get(nm, []):
+                if (wr or w2) and meet(cs, c2):
                     deps.add(j)
-        for (nm, lo, hi), wr in acc:
+        for (nm, cs), wr in acc:
             lst = last.setdefault(nm, [])
-            if wr:
-                lst[:] = [e for e in lst if not (lo <= e[0] and e[1] <= hi)]
-            lst.append((lo, hi, i, wr))
+            if wr and cs[2] == 1:
+                lst[:] = [e for e in lst if not (cs[0] <= e[0][0] and e[0][1] <= cs[1])]
+            lst.append((cs, i, wr))
         deps.discard(i)
         typ = "x" if kind != "c" else "s" if any("win" in x for x in writes) else "g" if any("win" in x for x in reads) else "c"
         cost *= PLANF.get(typ, 1.0)
@@ -209,11 +228,24 @@ def rank_program(g, core, T, topo):
         c = 0.065 + (i["n"] * 1.56 if "win" in i else max(64, i["n"])) * CYC
         return op("A", fn, [i] + cols(bias, scale), [o] + cols(accum), c)
 
-    def mm(lst, first=True, final=True, each=False):
+    def lin(eng, o, i, scale=None, bias=None):
+        if eng == "G":
+            return pick(o, i, [[0, o["n"]]], 0, 0)
+        if eng == "A":
+            return act(o, i, ACT.Identity, 0.0 if bias is None else bias, 1.0 if scale is None else scale)
+        if scale is None and bias is None:
+            return copy(o, i)
+        if bias is None:
+            return ts(o, i, scale, ALU.mult)
+        if scale is None:
+            return ts(o, i, bias, ALU.add)
+        return ts(o, i, scale, ALU.mult, bias, ALU.add)
+
+    def mm(lst, first=True, final=True):
         def fn(q):
             ins = None
             for j, (o, l_, r_) in enumerate(lst):
-                ins = q.matmul(o["ap"], l_["ap"], r_["ap"], each or (first and j == 0), each or (final and j == len(lst) - 1))
+                ins = q.matmul(o["ap"], l_["ap"], r_["ap"], first and j == 0, final and j == len(lst) - 1)
             return ins
         c = sum(max(64, r_["n"]) * (4 if r_["sz"] == 4 else 1) for o, l_, r_ in lst) * PEC
         return op("P", fn, [x for e in lst for x in e[1:]], [e[0] for e in lst], c)
@@ -224,6 +256,9 @@ def rank_program(g, core, T, topo):
         else:
             fn = lambda q: q.iota(o["ap"], pat, base, cm)
         return op("G", fn, [], [o], 0.13 + 2 * o["n"] * CYC)
+
+    def pick(o, i, pat, base, cm):
+        return op("G", lambda q: q.affine_select(o["ap"], i["ap"], pat, ALU.is_equal, 0.0, base, cm), [i], [o], 0.17 + 2 * o["n"] * CYC)
 
     def dma(eng, oap, iap, reads, writes, nbytes, after=()):
         return op(eng, lambda q: q.dma_start(oap, iap), reads, writes, 2.0 + nbytes / 150e3, "d", after)
@@ -252,16 +287,34 @@ def rank_program(g, core, T, topo):
         return s
 
     def top64(nm, lo, hi):
-        return {"ap": T[nm][0:64, lo:hi], "r": [(nm, lo, hi)], "n": hi - lo, "sz": 2, "ps": False}
+        return view(T[nm][0:64, lo:hi], nm, lo, hi, hi - lo)
 
     def eqp(b_, lo, hi):
-        return {"ap": T.eq[:, b_, lo:hi], "r": [("eq", 256 * b_ + lo, 256 * b_ + hi)], "n": hi - lo, "sz": 2, "ps": False}
+        return view(T.eq[:, b_, lo:hi], "eq", 256 * b_ + lo, 256 * b_ + hi, hi - lo)
 
-    def C(j):
-        return a("col", j, j + 1)
+    at = {}
+
+    def C(name, n=1):
+        if name not in at:
+            at[name] = sum(at.get("_n", []))
+            at.setdefault("_n", []).append(n)
+        return a("col", at[name], at[name] + n)
+
+    def Ct(name, t):
+        return a("col", at[name] + t, at[name] + t + 1)
 
     def M(j):
         return a("mask", j, j + 1)
+
+    def mat(j):
+        return a("mat", 128 * j, 128 * j + 128)
+
+    def big(nm, a_, base=0):
+        return a(nm, base + 15 - a_, base + 143 - a_)
+
+    def kc_rows(lo, hi, src):
+        js = [dma("S", T.KC[j:128:16, lo:hi], T[src][j:128:16, lo:hi], [a(src, lo, hi), a("KC", lo, hi)], [], 40e3) for j in range(6)]
+        last["KC"] = [e for e in last["KC"] if e[1] not in js] + [((lo, hi, 1), j, True) for j in js]
 
     dma("S", T.kin32[:, 0:576], T.kin[:, 0:576], [], [a("kin32", 0, 576)], 300e3)
     dma("A", T.kin32[:, 576:B], T.kin[:, 576:B], [], [a("kin32", 576, B)], 300e3)
@@ -271,33 +324,32 @@ def rank_program(g, core, T, topo):
 
     iota(a("pI", 0, 1), [[1, 1]], 0, 1, False)
     iota(a("inp"), [[1, 160]], -16, -1)
-    iota(a("inn"), [[1, 320]], 0, 0)
+    iota(a("inn"), [[1, 144]], 0, 0)
     ts(a("pI", 1, 2), a("pI", 0, 1), 15, ALU.bitwise_and)
     ts(a("pI", 2, 3), a("pI", 0, 1), 112, ALU.bitwise_and)
     ts(a("pI", 3, 4), a("pI", 0, 1), 16, ALU.bitwise_and)
-    copy(a("col", 0, 3), a("pI", 0, 3))
-    ts(C(3), C(2), 15.0, ALU.add)
-    ts(C(4), a("pI", 3, 4), 0.0625, ALU.mult)
-    ts(C(5), C(4), -1.0, ALU.mult, 1.0, ALU.add)
-    ts(a("E0"), a("inp"), 0.0, ALU.is_equal, C(5), ALU.mult)
-    ts(a("E1"), a("inp"), 0.0, ALU.is_equal, C(4), ALU.mult)
-    ts(a("mask"), a("inn", 0, 16), C(1), ALU.is_equal)
-    ts(a("Big"), a("inn", 0, 144), C(3), ALU.is_equal)
-    ts(C(10), C(1), 16.0, ALU.mult)
-    ts(a("lPerm"), a("inn", 0, 16), C(10), ALU.add)
-    ts(a("Id"), a("inp", 16, 144), 0.0, ALU.is_equal)
+    copy(C("p", 3), a("pI", 1, 4))
+    row, g16, odd16 = Ct("p", 0), Ct("p", 1), Ct("p", 2)
+    ts(C("end"), g16, 15.0, ALU.add)
+    ts(C("odd"), odd16, 0.0625, ALU.mult)
+    ts(C("even"), odd16, 0.0, ALU.is_equal)
+    ts(a("E0"), a("inp"), 0.0, ALU.is_equal, C("even"), ALU.mult)
+    ts(a("E1"), a("inp"), 0.0, ALU.is_equal, C("odd"), ALU.mult)
+    ts(a("mask"), a("inn", 0, 16), row, ALU.is_equal)
+    ts(a("Big"), a("inn"), C("end"), ALU.is_equal)
+    ts(C("r16"), row, 16.0, ALU.mult)
+    ts(a("lPerm"), a("inn", 0, 16), C("r16"), ALU.add)
+    sq = a("inp", 16, 144)
+    ts(a("Id"), sq, 0.0, ALU.is_equal)
     act(a("nId"), a("Id"), scale=-1.0)
     act(a("BigC"), a("Big"), scale=BIGK)
-    act(a("Bigf"), a("Big"))
+    act(a("BigN"), a("Big"), scale=-512.0)
     iota(a("KC", 0, B), [[0, B // 4], [1, 4]], 0, 0)
-    iota(a("kcon"), [[1, 16], [0, 16]], 0, 0)
-    iota(a("ing"), [[16, 8], [0, 16]], 0, 0)
-
-    def big(nm, a_, base=0):
-        return a(nm, base + 15 - a_, base + 143 - a_)
+    iota(a("iB"), [[1, 256]], 0, 0)
+    mset(a("one"), 1.0)
 
     def first_lists(t, bank):
-        copy(a("kvs", 256 * t, 256 * t + 256), a("kin32", t, 1024, 4))
+        lin("G" if t else "V", a("kvs", 256 * t, 256 * t + 256), a("kin32", t, 1024, 4))
         for bp in range(8):
             for c in range(2):
                 o = a(bank, 32 * bp + 16 * c, 32 * bp + 16 * c + 16)
@@ -312,15 +364,30 @@ def rank_program(g, core, T, topo):
         op("V", lambda q: q.transpose(o["ap"], i["ap"]), [i], [o], vcost([i], o))
         copy(a("off1", 256 * t, 256 * t + 256), ind(o, a("lPerm")))
 
-    first_lists(0, "P6")
-    copy(a("K0f"), a("kin32"))
-    kc_ops = [dma("S", T.KC[16 * g_:16 * g_ + 6, 0:B], T.K0f[16 * g_:16 * g_ + 6, :], [a("K0f"), a("KC", 0, B)], [], 60e3)
-              for g_ in range(8)]
-    last["KC"] = [(0, B, j, True) for j in kc_ops]
+    def repeat(nm, t):
+        for j in range(1, 4):
+            lo = 1024 * t + 256 * j
+            dma("S", T[nm][:, lo:lo + 256], T[nm][:, 1024 * t:1024 * t + 256], [a(nm, 1024 * t, 1024 * t + 256)], [a(nm, lo, lo + 256)], 65e3)
 
-    copy(a("col", 11, 14), a("w32", 0, 3))
+    def suitors(t):
+        lin("G", a("xv4", 1024 * t, 1024 * t + 256), a("X", t, 1024, 4))
+        repeat("xv4", t)
+        lin("G", a("kC4", 1024 * t, 1024 * t + 256), a("KC", t, 1024, 4))
+        repeat("kC4", t)
+
+    def own_features(t):
+        n0 = B + L * t
+        dma("S", T.X[:, n0:n0 + 320], T.xv4[:, 1024 * t:1024 * t + 320], [a("xv4", 1024 * t, 1024 * t + 320)], [a("X", n0, n0 + 320)], 80e3)
+
+    first_lists(0, "P6")
+    copy(a("K0f", 0, 576), a("kin32", 0, 576))
+    copy(a("K0f", 576, B), a("kin32", 576, B))
+    kc_rows(0, B, "K0f")
+    suitors(0)
+
+    copy(C("w", 3), a("w32", 0, 3))
     for t in range(R):
-        act(a("BigW", 144 * t, 144 * t + 144), a("Big"), scale=C(11 + t))
+        act(a("BigW", 144 * t, 144 * t + 144), a("Big"), scale=Ct("w", t))
         mm([(a("P7", 16 * t, 16 * t + 16), big("BigW", a_, 144 * t), a("X", 4 * a_ + t, 1024, 64)) for a_ in range(16)])
     copy(a("aI"), a("P7", 0, 48))
     ts(a("aJ"), a("aI"), 1023, ALU.bitwise_and)
@@ -330,280 +397,268 @@ def rank_program(g, core, T, topo):
     s1 = send("a1", [s1])
     s1 = send("a2", [s1])
     dma("S", T.Kf[:, 0:B], T.K0f[:, :], [a("K0f")], [a("Kf", 0, B)], 600e3, [ARR["a0"]])
+    own_features(0)
 
-    ts(C(6), C(1), 2.0, ALU.is_lt)
-    ts(C(7), C(1), 9.0, ALU.is_ge)
-    ts(C(8), C(1), 6.0, ALU.is_lt)
-    ts(C(9), C(1), 6.0, ALU.is_ge)
-    ts(a("col", 39, 42), a("inn", 0, 3), C(9), ALU.mult)
-    for t in range(R):
-        act(a("kC", 256 * t, 256 * t + 256), a("K0f", t, 1024, 4), bias=C(39 + t), scale=C(8))
-    sq = a("inp", 16, 144)
-    ts(a("P1a"), sq, 2.0, ALU.is_equal, C(6), ALU.mult)
-    ts(a("P1b"), sq, 1.0, ALU.is_equal, M(7), ALU.mult)
-    ts(a("P2a"), sq, 4.0, ALU.is_equal, C(6), ALU.mult)
-    act(a("P2b"), a("Id"), scale=C(7))
-    tt(a("P2a"), a("P2a"), a("P2b"), ALU.add)
-    ts(a("Pm1"), sq, 1.0, ALU.is_equal, M(0), ALU.mult)
-    ts(a("Pm6"), sq, 6.0, ALU.is_equal, M(0), ALU.mult)
-    act(a("hPm6"), a("Pm6"), scale=0.5)
-    act(a("hId"), a("Id"), scale=0.5)
-    ts(C(50), M(7), 2048.0, ALU.mult, M(6), ALU.add)
-    act(a("Big6"), a("Big"), scale=C(50))
-    tt(a("P1a"), a("P1a"), a("P1b"), ALU.add)
-    tt(a("P1a"), a("P1a"), a("nId"), ALU.add)
-    ts(a("BO"), a("ing"), C(2), ALU.is_equal)
+    iota(a("ing"), [[16, 8], [0, 16]], 0, 0)
+    iota(a("jm"), [[0, 16], [1, 16]], 0, 0)
+    iota(a("KC", B, W), [[0, (W - B) // 4], [1, 4]], 0, 0)
+    ts(a("BO"), a("ing"), g16, ALU.is_equal)
     act(a("BOo"), a("BO"), scale=65536.0)
-    iota(top64("Eg", 0, 1024), [[1, 64], [0, 16]], 0, -1)
-    ts(top64("Eg", 0, 1024), top64("Eg", 0, 1024), 0.0, ALU.is_equal)
-    act(a("o16"), a("Id"), bias=0.0625, scale=0.0)
-    iota(a("one"), [[0, 320]], 1, 0)
+    ts(a("diag"), a("jm"), row, ALU.is_equal)
+    ts(a("segm"), a("jm"), 0.0, ALU.is_gt)
+    ts(a("seg"), a("jm", 0, 64), 0.0, ALU.is_equal, 8388608.0, ALU.mult)
+    for q_ in range(4):
+        pick(a("Rs", 512 * q_, 512 * q_ + 512), a("one"), [[-1, 4], [-16, 8], [0, 16]], -4 * q_, 1)
+    for h in range(2):
+        pick(top64("Eg", 512 * h, 512 * h + 512), top64("one", 0, 512), [[-1, 32], [0, 16]], -32 * h, 1)
+    mset(a("o16"), 0.0625)
     iota(a("wed", 256, 320), [[0, 64]], 0, 0)
-    ts(a("lP15"), a("inn", 0, 16), 0.0, ALU.mult, C(1), ALU.add)
-    for a_ in range(16):
-        act(a("Rs", 128 * a_, 128 * a_ + 128), a("BO"), scale=M(a_))
+    ts(a("lP15"), a("inn", 0, 16), 0.0, ALU.mult, row, ALU.add)
     mset(a("tl", 0, 16), 0.5)
     mset(a("tl", 16, 32), 0.0)
     scan(a("pw", 0, 16), a("tl", 0, 16), a("tl", 16, 32), 131072.0, ALU.mult, ALU.add)
     copy(a("thrB"), ind(a("pw", 0, 16), a("lP15")))
     ts(a("tl", 16, 32), a("mask"), 0.5, ALU.mult)
     tt(a("pw", 16, 32), a("pw", 0, 16), a("tl", 16, 32), ALU.mult)
-    red(C(14), a("pw", 16, 32))
-    act(a("BOd"), a("BO"), scale=C(14))
-    iota(a("iB"), [[1, 256]], 0, 0)
-    ts(a("col", 51, 55), a("inn", 0, 4), C(9), ALU.mult)
-    iota(a("tl", 32, 48), [[64, 16]], 0, 0)
-    ts(C(15), C(1), 4.0, ALU.mult)
+    red(C("pw"), a("pw", 16, 32))
+    act(a("BOd"), a("BO"), scale=C("pw"))
+    iota(a("nI"), [[L, R], [16, 16]], B, 0)
+    ts(a("nL"), a("nI"), row, ALU.add)
     for t in range(R):
-        ts(a("vT", 16 * t, 16 * t + 16), a("tl", 32, 48), C(15), ALU.add, float(t), ALU.add)
         iota(a("D%d" % t, 256, 320), [[0, 64]], 0, 0)
-        iota(a("xvS", 320 * t + 256, 320 * t + 320), [[0, 64]], 0, 0)
-        act(a("xvS", 320 * t, 320 * t + 256), a("X", t, 1024, 4))
+        iota(a("cW", 272 * t + 256, 272 * t + 272), [[0, 16]], -1, 0)
     iota(a("rs"), [[256, 4], [1, 16]], 0, 0)
-    ts(a("pos"), a("rs"), C(10), ALU.add)
-    iota(a("seg"), [[0, 4], [1, 16]], 0, 0)
-    ts(a("seg"), a("seg"), 0.0, ALU.is_equal, 8388608.0, ALU.mult)
-    ts(a("scol", 0, 4), a("inn", 0, 64, 16), C(1), ALU.add, -0.5, ALU.add)
-    tt(C(16), M(6), M(7), ALU.add)
-    ts(C(17), C(16), -1.0, ALU.mult, 1.0, ALU.add)
-    ts(C(18), M(6), 4.0, ALU.mult, M(7), ALU.add)
-    ts(C(19), M(0), 4.0, ALU.mult, C(16), ALU.add)
-    ts(C(20), M(6), -1.0, ALU.mult, 1.0, ALU.add)
+    ts(a("pos"), a("rs"), C("r16"), ALU.add)
+    ts(a("scol", 0, 4), a("inn", 0, 64, 16), row, ALU.add, -0.5, ALU.add)
+    act(a("hId"), a("Id"), scale=0.5)
     t3 = a("inn", 0, 3)
-    ts(C(42), M(7), float(L), ALU.mult, M(6), ALU.add)
-    ts(C(43), M(7), float(B), ALU.mult)
-    ts(a("col", 24, 27), t3, C(42), ALU.mult, C(43), ALU.add)
-    ts(C(44), C(16), float(L), ALU.mult, M(0), ALU.add)
-    ts(C(45), C(16), float(B), ALU.mult)
-    ts(a("col", 27, 30), t3, C(44), ALU.mult, C(45), ALU.add)
-    ts(a("col", 46, 49), t3, float(L), ALU.mult, float(B), ALU.add)
-    ts(a("col", 30, 33), a("col", 46, 49), C(20), ALU.mult)
-    ts(a("col", 33, 36), a("mask", 9, 12), C(16), ALU.subtract, -1000.0, ALU.mult)
-    ts(C(49), C(16), -499.0, ALU.mult, -1.0, ALU.add)
-    ts(a("col", 36, 39), a("mask", 9, 12), 64.5, ALU.mult, C(49), ALU.add)
+    ts(C("lt2"), row, 2.0, ALU.is_lt)
+    ts(C("lt9"), row, 9.0, ALU.is_lt)
+    ts(C("r911"), row, 12.0, ALU.is_lt, C("lt9"), ALU.subtract)
+    ts(C("m67"), M(6), M(7), ALU.add)
+    ts(C("n67"), C("m67"), -1.0, ALU.mult, 1.0, ALU.add)
+    ts(C("d5"), C("m67"), C("r911"), ALU.add)
+    ts(C("s1a"), C("lt2"), 2.0, ALU.mult, M(7), ALU.add)
+    ts(C("s1"), M(6), 6.0, ALU.mult, C("s1a"), ALU.add)
+    ts(C("w1"), C("lt2"), M(7), ALU.add, M(6), ALU.subtract)
+    ts(mat(0), sq, C("s1"), ALU.is_equal, C("w1"), ALU.mult)
+    act(mat(1), a("nId"), scale=C("d5"))
+    ts(C("m1c"), M(1), M(12), ALU.add)
+    act(mat(2), a("Id"), scale=C("m1c"))
+    ts(a("A3", 0, 128), sq, 4.0, ALU.is_equal, C("lt2"), ALU.mult)
+    act(a("A3", 128, 256), a("nId"), scale=C("lt9"))
+    tt(a("A3", 0, 128), a("A3", 0, 128), a("A3", 128, 256), ALU.add)
+    act(mat(3), a("Id"), scale=C("lt9"))
+    act(mat(4), a("Id"), scale=C("m67"))
+    ts(C("s6"), M(12), -6.0, ALU.mult)
+    ts(C("w6"), M(12), M(7), ALU.add, C("r911"), ALU.add)
+    ts(mat(5), sq, C("s6"), ALU.is_equal, C("w6"), ALU.mult)
+    ts(C("w7"), C("r911"), -1001.0, ALU.mult, 1.0, ALU.add)
+    act(mat(6), a("Id"), scale=C("w7"))
+    act(mat(7), a("nId"), scale=C("r911"))
+    ts(C("f0"), C("r911"), 4999.5, ALU.mult, 0.5, ALU.add)
+    ts(C("f", 3), a("mask", 9, 12), -5063.5, ALU.mult, C("f0"), ALU.add)
+    ts(C("ca"), M(0), 4.0, ALU.mult, C("d5"), ALU.add)
+    ts(C("cb1"), C("d5"), float(L), ALU.mult, M(0), ALU.add)
+    ts(C("cb0"), C("d5"), float(B), ALU.mult)
+    ts(C("cb", 3), t3, C("cb1"), ALU.mult, C("cb0"), ALU.add)
+    ts(C("cc"), M(6), 4.0, ALU.mult, M(7), ALU.add)
+    ts(C("cd1"), M(7), float(L), ALU.mult, M(6), ALU.add)
+    ts(C("cd0"), M(7), float(B), ALU.mult)
+    ts(C("cd", 3), t3, C("cd1"), ALU.mult, C("cd0"), ALU.add)
     for t in range(R):
-        act(a("DD", 256 * t, 256 * t + 128), a("Id"), scale=C(33 + t))
-        act(a("DD", 256 * t + 128, 256 * t + 256), a("nId"), scale=M(9 + t))
-    s8 = {"ap": T.s8[0:8, :], "r": [("s8", 0, 128)], "n": 128, "sz": 4, "ps": False}
-    op("G", lambda q: q.iota(s8["ap"], [[1, 8], [0, 16]], 0, -1, allow_small_or_imprecise_dtypes=True), [], [s8], 0.4)
-    ts(s8, s8, 0.0, ALU.is_equal, 16.0, ALU.mult)
-    thi = {"ap": T.th32[0:8, 0:3], "r": [("th32", 0, 3)], "n": 3, "sz": 4, "ps": False}
-    thf = {"ap": T.thf[0:8, 0:3], "r": [("thf", 0, 3)], "n": 3, "sz": 4, "ps": False}
-    copy(thf, thi)
+        lin("V", a("cv", 256 * t, 256 * t + 256), a("iB"), C("ca"), Ct("cb", t))
+        lin("A", a("cvn", 256 * t, 256 * t + 256), a("iB"), C("cc"), Ct("cd", t))
+    s8 = view(T.s8[0:8, :], "s8", 0, 128, 128)
+    iota(s8, [[1, 8], [0, 16]], 0, -1)
+    ts(s8, s8, 0.0, ALU.is_equal, 512.0, ALU.mult)
+    thf = view(T.thf[0:8, 0:3], "thf", 0, 3, 3)
+    ts(thf, view(T.th32[0:8, 0:3], "th32", 0, 3, 3), 4081.0, ALU.min)
     mm([(a("P7", 64, 67), s8, thf)])
-    copy(a("col", 21, 24), a("P7", 64, 67))
+    copy(C("th", 3), a("P7", 64, 67))
 
-    def scores(t, k0, k1, dyn, banks, kdst, cdst):
+    def scores(t, s0, block, late, banks):
+        ks, l1, how, kw = block
         bd0, bd1, bc, bk = banks
-        n = k1 - k0
-        P = B + L * t if dyn else B
-        base = 4096 * (t & 1)
-        o1 = 256 * t
-        onA = A_ON_SCALAR.get((t, k0))
-        late = dyn and t > 0
-        ks = [k for k in range(k0, k1) if k not in (6, 7)] + [6, 7] if late else list(range(k0, k1))
-        if late:
-            bc = bk
-        for s0, s1 in ([(0, n - 2), (n - 2, n)] if late else [(0, n)]):
-            if late and s0:
-                late_lists(t)
-            for s_ in range(s0, s1):
+        n = len(ks)
+        P = B + L * t if late else B
+        base = 4096 * (t & 1) + 256 * s0
+        o1, o2 = 256 * t, 256 * t + 16 * s0
+
+        def part(nm, u, v):
+            return a(nm, base + 256 * u, base + 256 * v)
+
+        def turn(o, w_, nm, u, v):
+            return [(o, big(w_, a_), a(nm, base + 256 * u + a_, base + 256 * v, 16)) for a_ in range(16)]
+
+        for u, v in ([(0, n - 2), (n - 2, n)] if late else [(0, n)]):
+            for s_ in range(u, v):
                 k = ks[s_]
-                off = a("off1", o1 + 16 * k, o1 + 16 * k + 16)
-                mk = M((k + t) & 15)
-                if onA is not None:
-                    act(a("Gf", onA + 256 * s_, onA + 256 * s_ + 256), ind(a("K0f"), off), scale=mk)
-                else:
-                    win = a("Kf", 0, P) if late else a("kin32")
-                    ts(a("G", base + 256 * (k0 + s_), base + 256 * (k0 + s_ + 1)), ind(win, off), mk, ALU.mult)
-            o = a(bc, 0, 16 * (s1 - s0))
-            if onA is not None:
-                mm([(o, big("Bigf", a_), a("Gf", onA + a_, onA + 256 * n, 16)) for a_ in range(16)])
+                win = a("Kf", 0, P) if late else a("kin32" if l1[s_] == "V" else "K0f")
+                lin(l1[s_], part("G", s_, s_ + 1), ind(win, a("off1", o1 + 16 * k, o1 + 16 * k + 16)), M((k + t) & 15))
+            mm(turn(a(bc, 0, 16 * (v - u)), "Big", "G", u, v))
+            copy(a("off2", o2 + 16 * u, o2 + 16 * v), a(bc, 0, 16 * (v - u)))
+            for x, y in runs(ks[u:v]):
+                k = ks[u + x]
+                lin(CFG["c"], a("cW", 272 * t + 16 * k, 272 * t + 16 * (k + y - x)), a(bc, 16 * x, 16 * y))
+            for x in range(u, v, kw):
+                y = min(x + kw, v)
+                tt(part("Cq", x, y), ind(a("KC", 0, P), a("off2", o2 + 16 * x, o2 + 16 * y)),
+                   a("kC4", 1024 * t, 1024 * t + 256 * (y - x)), ALU.is_equal)
+        mm(turn(a(bk, 0, 16 * n), "BigC", "Cq", 0, n)
+           + [(a(bk, 16 * u, 16 * v), a("Id"), a("iB", 16 * ks[u], 16 * (ks[u] + v - u))) for u, v in runs(ks)], True, False)
+        cuts = [max(0, n - 2 * j) for j in range(len(how), -1, -1)]
+        pairs = list(zip(cuts, cuts[1:], how))
+        same = [[pairs[0]]]
+        for p_ in pairs[1:]:
+            if p_[2] == same[-1][0][2]:
+                same[-1].append(p_)
             else:
-                mm([(o, big("Big", a_), a("G", base + 256 * (k0 + s0) + a_, base + 256 * (k0 + s1), 16)) for a_ in range(16)])
-            copy(a("off2", o1 + 16 * (k0 + s0), o1 + 16 * (k0 + s1)), o)
-            act(a(cdst[0], cdst[1] + 16 * s0, cdst[1] + 16 * s1), o)
-        for k in range(k0, k1):
-            tt(a("Cq", base + 256 * k, base + 256 * k + 256), ind(a("KC", 0, P), a("off2", o1 + 16 * k, o1 + 16 * k + 16)),
-               a("kC", 256 * t, 256 * t + 256), ALU.is_equal)
-        xv = a("xvS", 320 * t, 320 * t + 256)
-        for j, k in enumerate(range(k0, k1, 2)):
-            ke = min(k + 2, k1)
-            bank = (bd0, bd1)[j & 1]
-            w_ = 256 * (ke - k)
-            xc = a("xc", base + 256 * k, base + 256 * ke)
-            (copy if late and (t, j) in XC_ON_V else act)(xc, ind(a("X", 0, P), a("off2", o1 + 16 * k, o1 + 16 * ke)))
-            mm([(a(bank, 0, w_), a("Id"), xc)] + [(a(bank, 256 * u, 256 * u + 256), a("nId"), xv) for u in range(ke - k)])
-            act(a("ad", base + 256 * k, base + 256 * ke), a(bank, 0, w_), ACT.Abs, scale=16.0)
-        o = a(bk, 0, 16 * n)
-        runs = [(0, n - 3), (n - 3, n - 2), (n - 2, n)] if late else [(0, n)]
-        mm([(o, big("BigC", a_), a("Cq", base + 256 * k0 + a_, base + 256 * k1, 16)) for a_ in range(16)]
-           + [(a(bk, 16 * u, 16 * v), a("Id"), a("kcon", 16 * ks[u], 16 * (ks[u] + v - u))) for u, v in runs], True, False)
-        mm([(o, big("Big", a_), a("ad", base + 256 * k0 + a_, base + 256 * k1, 16)) for a_ in range(16)], False, True)
-        if dyn:
-            copy(kdst, o)
+                same.append([p_])
+        xv = a("xv4", 1024 * t, 1024 * t + 256)
+        for j, grp in enumerate(same):
+            u, v = grp[0][0], grp[-1][1]
+            o = a(bk, 16 * u, 16 * v)
+            end = j == len(same) - 1
+            if grp[0][2] == "a":
+                for x, y, _ in grp:
+                    bank = (bd0, bd1)[(n - x) // 2 & 1]
+                    w_ = 256 * (y - x)
+                    act(part("xc", x, y), ind(a("X", 0, P), a("off2", o2 + 16 * x, o2 + 16 * y)))
+                    mm([(a(bank, 256 * z, 256 * z + 256), a("nId"), xv) for z in range(y - x)] + [(a(bank, 0, w_), a("Id"), part("xc", x, y))])
+                    act(part("ad", x, y), a(bank, 0, w_), ACT.Abs, scale=512.0)
+                mm(turn(o, "Big", "ad", u, v), False, end)
+            else:
+                for x in range(u, v, kw):
+                    y = min(x + kw, v)
+                    tt(part("ad", x, y), ind(a("X", 0, P), a("off2", o2 + 16 * x, o2 + 16 * y)),
+                       a("xv4", 1024 * t, 1024 * t + 256 * (y - x)), ALU.subtract)
+                ts(part("xc", u, v), part("ad", u, v), 0.0, ALU.max, -2.0, ALU.mult)
+                mm(turn(o, "BigN", "ad", u, v), False, False)
+                mm(turn(o, "BigN", "xc", u, v), False, end)
+
+    def least(t, j, bank):
+        n = len(BLOCKS[t][j][0])
+        w_ = 16 * min(n, 4)
+        b_ = a("best", 64 * t, 64 * t + w_)
+        if j == 0:
+            ts(b_, a(bank, 0, w_), NONE, ALU.min)
         else:
-            act(kdst, o)
+            tt(b_, a(bank, 0, w_), b_, ALU.min)
+        if j == len(BLOCKS[t]) - 1:
+            tt(a("td", 0, 32), a("best", 64 * t, 64 * t + 32), a("best", 64 * t + 32, 64 * t + 64), ALU.min)
+            if n > 4:
+                tt(a("td", 0, 16), a(bank, 64, 80), a("td", 0, 16), ALU.min)
+            tt(a("km"), a("td", 0, 16), a("td", 16, 32), ALU.min)
 
     def late_lists(t):
-        mm([(a("P7", 0, 16), big("Big6", a_), a("kvd", 256 * t + a_, 256 * t + 256, 16)) for a_ in range(16)])
-        copy(a("oi", 0, 16), a("P7", 0, 16))
-        ts(a("oi", 16, 32), a("oi", 0, 16), 2047, ALU.bitwise_and)
-        ts(a("oi", 32, 48), a("oi", 0, 16), 11, ALU.logical_shift_right)
-        copy(a("off1", 256 * t + 96, 256 * t + 128), a("oi", 16, 48))
+        for j in range(2):
+            lin(CFG["kv2"][j], view(T.kv2[:, j, :], "kv2", 256 * j, 256 * j + 256, 256), a("Kf", t, 1024, 4), M(6 + j))
+        mm([(a("P6", 0, 32), big("Big", a_), view(T.kv2[:, :, a_:256:16], "kv2", 0, 512, 32)) for a_ in range(16)])
+        copy(a("off1", 256 * t + 96, 256 * t + 128), a("P6", 0, 32))
 
-    def tree(src, lo, n, tmp, dst, f):
-        cur, cl, at = src, lo, 0
-        while n > 1:
-            h = (n + 1) // 2
-            o = dst if h == 1 else a(tmp, at, at + 16 * h)
-            tt(o, a(cur, cl, cl + 16 * h), a(cur, cl + 16 * (n - h), cl + 16 * n), f)
-            cur, cl, at, n = tmp, at, at + 16 * h, h
-
-    def argmin(kn, cn_, lo, n, kdst, cps, t0, t1, t2):
-        tree(kn, lo, n, t0, kdst, ALU.min)
-        e = a(t1, 0, 16 * n)
-        tt(e, ind(kdst, a("lP15", 0, n)), a(kn, lo, lo + 16 * n), ALU.is_equal)
-        tt(a(t2, 0, 16 * n), e, a(cn_, lo, lo + 16 * n), ALU.mult)
-        mm([(cps, a("Id"), a(t2, 16 * j, 16 * j + 16)) for j in range(n)])
-
-    STAT = [[(0, 4), (4, 8), (8, 12)], [(0, 5), (9, 13), (13, 16)], [(0, 4), (9, 13), (13, 16)]]
-    DYN = [(12, 16), (5, 9), (4, 9)]
-    SB, DB = ("P0", "P1", "P2", "P3"), ("P4", "P5", "P6", "P7")
+    SB = ("P0", "P0", "P2", "P3")
 
     def static_part(t):
-        at = 192 * t
-        for (k0, k1) in STAT[t]:
-            n = 16 * (k1 - k0)
-            scores(t, k0, k1, False, SB, a("key1", at, at + n), ("c1", at))
-            at += n
-        argmin("key1", "c1", 192 * t, (at - 192 * t) // 16, a("key2", 96 * t, 96 * t + 16), a("P3", 0, 16), "ta", "tb", "tc")
-        act(a("c2", 96 * t, 96 * t + 16), a("P3", 0, 16))
+        for j in range(3):
+            banks = SB if t else (("P0", "P1", "P2", "P3"), ("P4", "P5", "P6", "P7"))[j & 1]
+            scores(t, 4 * j, BLOCKS[t][j], False, banks)
+            least(t, j, banks[3])
 
     def dynamic_part(t):
         n0 = B + L * t
-        c0 = 24 + 8 * t
-        k0, k1 = DYN[t]
-        nd = k1 - k0
-        act(a("DS%d" % t), ind(a("Kf" if t else "K0f", 0, 1024), a("aR%d" % t)))
+        lastr = t == R - 1
+        lin(CFG["DS"][t], a("DS%d" % t), ind(a("Kf" if t else "K0f", 0, 1024), a("aR%d" % t)))
         sd = send("d%d" % t)
         if t == 0:
             send("xs2", [sd])
             send("xs1", [sd])
             kv = a("kvs", 0, 256)
-            thr = C(21)
+            thr = Ct("th", 0)
         else:
             kv = a("kvd", 256 * t, 256 * t + 256)
-            copy(kv, a("Kf", t, 1024, 4))
+            lin("G", kv, a("Kf", t, 1024, 4))
             thr = a("thr", t, t + 1)
-        scores(t, k0, k1, True, DB, a("key2", 96 * t + 16, 96 * t + 16 + 16 * nd), ("c2", 96 * t + 16))
-        argmin("key2", "c2", 96 * t, nd + 1, a("km"), a("P6", 0, 16), "td", "te", "tf")
-        ts(a("iv"), a("km"), BIGK, ALU.is_ge, -4096.0, ALU.mult)
-        ts(a("nc"), a("km"), thr, ALU.is_ge, 2047.0, ALU.mult)
-        tt(a("mH"), a("P6", 0, 16), a("nc"), ALU.max)
-        tt(a("mS"), a("P6", 0, 16), a("iv"), ALU.add)
-        mm([(a("P5", a_, 256, 16), a("Rs", 128 * a_, 128 * a_ + 128), a("mH")) for a_ in range(16)], each=True)
-        copy(a("mB"), a("P5", 0, 256))
-        ts(a("En"), a("mB"), 2047.0, ALU.is_equal, 4096.0, ALU.mult)
-        mm([(a("P7", 0, 256), a("BO"), a("En"))], True, False)
+        lin("G", a("Kf", n0, n0 + L), a("Kf", t, 1024, 4))
+        s0 = sum(len(b_[0]) for b_ in BLOCKS[t][:3])
+        scores(t, s0, BLOCKS[t][3], t > 0, ("P4", "P5", "P7", "P7") if t else ("P4", "P5", "P6", "P7"))
+        least(t, 3, "P7")
+        ts(a("wi"), a("km"), 511, ALU.bitwise_and)
+        copy(a("wl"), a("wi"))
+        ts(a("nc"), a("km"), thr, ALU.is_ge, 65536.0, ALU.mult)
+        tt(a("Em"), ind(a("cW", 272 * t, 272 * t + 272), a("wl")), a("diag"), ALU.mult)
+        mm([(a("P5", 0, 256), a("BO"), a("Em"))])
+        lin(CFG["mB"][t], a("mB"), a("P5", 0, 256))
+        mS = a("mS", 15, 256, 16)
+        if CFG["mS"][t] == "V":
+            scan(a("mS"), a("segm"), a("Em"), 0.0, ALU.mult, ALU.add)
+        else:
+            mm([(a("P6", 0, 16), a("Id"), a("Em", a_, 256, 16)) for a_ in range(16)])
+            act(mS, a("P6", 0, 16))
+        mm([(a("P7", a_, 256, 16), a("Rs", 128 * a_, 128 * a_ + 128), a("nc")) for a_ in range(16)], True, False)
         for b_ in range(16):
-            ts(eqp(b_, 0, 256 - 16 * b_), a("mB", 16 * b_, 256), a("mS", b_, b_ + 1), ALU.is_equal)
+            ts(eqp(b_, 0, 256 - 16 * b_), a("mB", 16 * b_, 256), a("mS", 16 * b_ + 15, 16 * b_ + 16), ALU.is_equal)
             if b_ < 15:
                 mm([(a("P7", 16 * b_ + 16, 256), a("BOo"), eqp(b_, 16, 256 - 16 * b_))], False, False)
-        mm([(a("P7", 0, 256), a("BOd"), {"ap": T.eq[:, :, 0:16], "r": [("eq", 0, 4096)], "n": 256, "sz": 2, "ps": False})], False, True)
-        tt(a("dmv"), a("mS"), a("vT", 16 * t, 16 * t + 16), ALU.subtract)
-        ts(a("dmv"), a("dmv"), 0.0625, ALU.mult)
-        ts(a("cn"), a("iB"), C(20), ALU.mult, C(30 + t), ALU.add)
-        ts(a("cv2"), a("iB"), C(19), ALU.mult, C(27 + t), ALU.add)
-        act(a("cvn"), a("iB"), bias=C(24 + t), scale=C(18))
-        mm([(a("P4", 0, 256), a("Pm6"), a("mB")), (a("P4", 0, 256), a("Id"), a("cn")), (a("P4", 0, 256), a("nId"), kv)])
+        mm([(a("P7", 0, 256), a("BOd"), view(T.eq[:, :, 0:16], "eq", 0, 4096, 256))], False, True)
+        mm([(a("P4", 0, 256), l_, r_) for l_, r_ in ((mat(0), kv), (mat(1), kv), (mat(2), a("mB")), (a("Id"), a("cv", 256 * t, 256 * t + 256)))], True, False)
         wed = a("wed", 0, 256)
         tt(wed, a("P7", 0, 256), a("thrB"), ALU.is_lt)
-        mm([(a("P6", 0, 16), big("Big", a_), a("wed", a_, 256, 16)) for a_ in range(16)])
-        scan(a("cum"), a("one"), a("wed"), -1.0, ALU.add, ALU.subtract)
-        nv = 2 if t in COUNT_ON_V else 0
+        mm([(a("P6", 0, 16), a("Id"), a("nL", 16 * t, 16 * t + 16))] + [(a("P6", 0, 16), big("BigN", a_), a("wed", a_, 256, 16)) for a_ in range(16)])
+        scan(a("cum"), a("one", 0, 320), a("wed"), -1.0, ALU.add, ALU.subtract)
+        tt(a("ms"), a("P6", 0, 16), mS, ALU.max)
+        copy(a("msl"), a("ms"))
+        nv = CFG["count"][t]
         for c in range(nv):
             ts(a("jv", 320 * c, 320 * c + 320), a("cum"), a("scol", c, c + 1), ALU.is_lt, 0.5, ALU.subtract)
             red(a("acc", c, c + 1), a("jv", 320 * c, 320 * c + 320))
         for c in range(nv, 4):
-            act(a("junk"), a("cum"), ACT.Sign, a("scol", c, c + 1), -1.0, a("acc", c, c + 1))
-        tt(a("t1"), a("P6", 0, 16), a("dmv"), ALU.mult)
-        tt(a("t2"), a("t1"), a("vT", 16 * t, 16 * t + 16), ALU.add)
-        copy(a("msl"), a("t2"))
-        if t in KM_ON_V:
-            ts(a("kmz"), ind(a("Kf", 0, n0), a("msl")), C(17), ALU.mult)
-        else:
-            act(a("kmz"), ind(a("Kf", 0, n0), a("msl")), scale=C(17))
-        mm([(a("P5", 0, 256), a("DD", 256 * t, 256 * t + 128), wed), (a("P5", 0, 256), a("DD", 256 * t + 128, 256 * t + 256), a("cum", 0, 256))])
-        act(a("Fv"), a("P5", 0, 256), ACT.Sign, C(36 + t))
-        tt(a("prV"), a("P4", 0, 256), a("Fv"), ALU.mult)
-        o = a("P7", 0, 256)
-        mm([(o, a("P1a"), kv), (o, a("Pm1"), a("mB")), (o, a("Id"), a("cv2"))], True, False)
-        mm([(o, a("P2a"), a("kmz"))], False, True)
-        tt(ind(a("Kf", 0, n0), a("msl")), a("kmz"), a("cvn"), ALU.add)
-        mm([(a("P6", 0, 256), l_, r_) for l_, r_ in ((a("hPm6"), a("mB")), (a("hId"), a("cn")), (a("hId"), kv), (a("hId"), a("prV")))])
-        act(a("Kf", t, 1024, 4), a("P6", 0, 256))
-        tt(a("prC"), o, wed, ALU.mult)
-        mm([(o, a("Id"), a("prC")), (o, a("Id"), kv)])
-        act(a("Kf", n0, n0 + L), o)
-        if t < R - 1:
-            for r_ in range(4):
-                act(a("KC", n0 + r_, n0 + L, 4), a("Kf", n0 + r_, n0 + L, 4), bias=C(51 + r_), scale=C(8))
+            lo = 16 if c in (1, 2) else 0
+            act(a("junk", lo, 320 - lo), a("cum", lo, 320 - lo), ACT.Sign, a("scol", c, c + 1), -1.0, a("acc", c, c + 1))
+        lin(CFG["km"][t], a("kmz"), ind(a("Kf", 0, n0 + L), a("msl")), C("n67"))
+        mm([(a("P5", 0, 256), mat(6), wed), (a("P5", 0, 256), mat(7), a("cum", 0, 256))])
+        ts(a("Fv"), a("P5", 0, 256), Ct("f", t), ALU.is_gt)
+        mm([(a("P4", 0, 256), a("A3", 0, 128), a("kmz"))], False, True)
+        tt(ind(a("Kf", 0, n0 + L), a("msl")), a("kmz"), a("cvn", 256 * t, 256 * t + 256), ALU.add)
+        if not lastr:
+            late_lists(t + 1)
+        tt(a("Pr"), a("P4", 0, 256), a("Fv"), ALU.mult)
+        mm([(a("P7", 0, 256), mat(4), kv), (a("P7", 0, 256), mat(3), a("Pr"))])
+        mm([(a("P4", 0, 256), a("Id"), kv), (a("P4", 0, 256), mat(5), a("Pr"))])
+        tt(a("Kf", n0, n0 + L), a("P7", 0, 256), a("kmz"), ALU.add)
+        act(a("Kf", t, 1024, 4), a("P4", 0, 256))
+        if not lastr:
+            kc_rows(n0, n0 + L, "Kf")
         if t == 0:
             dma("S", T.yk[:, 0:B], T.K0f[:, :], [a("K0f")], [a("yk", 0, B)], 600e3, [ARR["xs2"], ARR["xs1"]])
         dma("S", T.yk[:, n0:n0 + L], T.Kf[:, n0:n0 + L], [a("Kf", n0, n0 + L)], [a("yk", n0, n0 + L)], 130e3)
         if t:
-            for row in ((9, 10), (6, 7, 11))[t - 1]:
-                hi = n0 if row < 9 else 1024
-                dma("S", T.yk[row:128:16, 0:hi], T.Kf[row:128:16, 0:hi], [a("Kf", 0, hi), a("yk", 0, hi)], [], 60e3)
-        act(a("sm"), ind(a("X", 0, n0), a("msl")))
-        mm([(a("P6", 256, 512), a("Id"), r_) for r_ in (a("xvS", 320 * t, 320 * t + 256), a("sm"))])
-        act(a("sy"), a("P6", 256, 512), bias=MAGIC, scale=0.4995)
-        act(a("X", n0, n0 + L), a("sy"), bias=-MAGIC)
+            for r_ in ((9, 10), (6, 7, 11))[t - 1]:
+                hi = n0 if r_ < 9 else 1024
+                dma("S", T.yk[r_:128:16, 0:hi], T.Kf[r_:128:16, 0:hi], [a("Kf", 0, hi), a("yk", 0, hi)], [], 60e3)
+        lin(CFG["sm"][t], a("sm"), ind(a("X", 0, n0 + L), a("msl")), None, -0.5)
+        mm([(a("P5", 256, 512), a("hId"), r_) for r_ in (a("xv4", 1024 * t, 1024 * t + 256), a("sm"))])
+        ts(a("X", n0, n0 + L), a("P5", 256, 512), MAGIC, ALU.add, MAGIC, ALU.subtract)
         if nv:
             ts(a("lan", 0, nv), a("acc", 0, nv), 160.0, ALU.add)
-        ts(a("lan", nv, 4), a("acc", nv, 4), 0.5, ALU.mult, 160.0, ALU.add)
+        if nv < 4:
+            ts(a("lan", nv, 4), a("acc", nv, 4), 0.5, ALU.mult, 160.0, ALU.add)
         lan = a("lan", 0, 4)
         copy(a("Dc"), ind(a("D%d" % t), lan))
-        act(a("xvc"), ind(a("xvS", 320 * t, 320 * t + 320), lan))
+        act(a("xvc"), ind(a("xv4", 1024 * t, 1024 * t + 320), lan))
         xqw = a("XQ%d" % t)
-        pt = {"ap": T.P5[0:64, 0:128], "r": [("P5", 0, 512)], "n": 128, "sz": 4, "ps": True}
+        b0, b1, b2 = ("P1", "P0", "P2") if lastr else ("P1", "P5", "P6")
+        pt = {"ap": T[b0][0:64, 0:128], "r": [(b0, (0, 512, 1))], "n": 128, "sz": 4, "ps": True}
         mm([(pt, a("xvc"), a("nId"))])
         act(top64("xvT", 0, 128), pt)
-        for h, bank in enumerate(("P5", "P4")):
+        for h, bank in enumerate((b0, b1)):
             mm([(a(bank), top64("xvT", 0, 128), top64("Eg", 512 * h, 512 * h + 512))], True, False)
             xq = a("xq", 512 * h, 512 * h + 512)
-            src = ind(xqw, a("Dc", 32 * h, 32 * h + 32))
-            if h == 0 or t in XQ_ON_A:
-                act(xq, src)
-            else:
-                copy(xq, src)
+            lin(CFG["xq"][t][h], xq, ind(xqw, a("Dc", 32 * h, 32 * h + 32)))
             mm([(a(bank), a("Id"), xq)], False, True)
-            aq = {"ap": T.aq[:, 2 * h:2 * h + 2, :], "r": [("aq", 512 * h, 512 * h + 512)], "n": 512, "sz": 2, "ps": False}
-            act(aq, a(bank), ACT.Abs, scale=1024.0)
-        o = a("P6", 0, 64)
-        mm([(o, a("Id"), a("pos"))] + [(o, big("Big", a_), {"ap": T.aq[:, :, 16 * a_:16 * a_ + 16], "r": [("aq", 0, 1024)], "n": 64, "sz": 2, "ps": False})
-                                       for a_ in range(16)])
+            act(view(T.aq[:, 2 * h:2 * h + 2, :], "aq", 512 * h, 512 * h + 512, 512), a(bank), ACT.Abs, scale=1024.0)
+        o = a(b2, 0, 64)
+        mm([(o, a("Id"), a("pos"))] + [(o, big("Big", a_), view(T.aq[:, :, 16 * a_:16 * a_ + 16], "aq", 0, 1024, 64)) for a_ in range(16)])
         scan(a("rs"), a("seg"), o, 0.0, ALU.add, ALU.min)
         copy(a("ri", 0, 4), a("rs", 15, 64, 16))
         ts(a("rj", 0, 4), a("ri", 0, 4), 1023, ALU.bitwise_and)
@@ -615,23 +670,25 @@ def rank_program(g, core, T, topo):
         if t == 1:
             send("xn12")
         dma("S", T.yx[:, L * t:L * t + L], T.X[:, n0:n0 + L], [a("X", n0, n0 + L)], [], 65e3)
-        if t < R - 1:
-            mm([(a("P6", 0, 1), a("o16"), a("cum", 255, 256))])
-            ts(a("zi", 0, 1), a("P6", 0, 1), -1.0, ALU.mult, 2040.0, ALU.add)
+        if not lastr:
+            own_features(t + 1)
+            mm([(a("P4", 0, 1), a("o16"), a("cum", 255, 256))])
+            ts(a("zi", 0, 1), a("P4", 0, 1), -1.0, ALU.mult, 2040.0, ALU.add)
             ts(a("zi", 1, 2), a("zi", 0, 1), 15, ALU.bitwise_and)
-            ts(a("thr", t + 1, t + 2), a("zi", 1, 2), 16.0, ALU.mult, C(22 + t), ALU.add)
+            ts(a("thr", t + 1, t + 2), a("zi", 1, 2), 512.0, ALU.mult, Ct("th", t + 1), ALU.add)
 
     static_part(0)
-    dynamic_part(0)
-    for t in (1, 2):
-        first_lists(t, "P2")
-        static_part(t)
+    for t in range(R):
+        if t < R - 1:
+            suitors(t + 1)
+            first_lists(t + 1, "P2")
         dynamic_part(t)
+        if t < R - 1:
+            static_part(t + 1)
 
     emit(ops, Q, T, sent[0])
 
 
-_S["yk"] = (W, F32)
 LOG = []
 PLAN = []
 ITER, NOISE = [3000], [0.5, 2.0, 4.0, 8.0, 14.0]
@@ -707,7 +764,7 @@ def emit(ops, Q, T, sent):
             vals = [replay(order, sc) for sc in SCALES]
             val = sum(math.log(v) for v in vals)
             if best is None or val < best[0]:
-                best = (val, order, st, vals)
+                best = (val, order, st, vals, max(pr))
             base = st if it % 4 else best[2]
             seq = sorted(range(n), key=lambda i: (-(base[i] + ops[i]["cost"]), -i))
             bt = place(seq, succ, True)

import math
from concourse.mybir import AluOpType, AxisListType, ActivationFunctionType

ALU = AluOpType
ACT = ActivationFunctionType
N, B, L, R, W = 4, 1152, 256, 3, 1920
BIGK = 4194304.0
NONE = 2097152.0 + 256.0
MAGIC = 12582912.0

F32, BF, F16, I32, U16 = "float32", "bfloat16", "float16", "int32", "uint16"
_S = {
    "kin32": (B, I32), "K0f": (B, F32), "Kf": (W, F32), "KC": (W, F32), "X": (W + 64, BF),
    "XQ0": (B, BF), "XQ1": (B + L, BF), "XQ2": (B + 2 * L, BF),
    "D0": (320, F32), "D1": (320, F32), "D2": (320, F32), "DS0": (L, F32), "DS1": (L, F32), "DS2": (L, F32),
    "aS": (48, U16), "aR0": (16, U16), "aR1": (16, U16), "aR2": (16, U16), "aI": (48, I32), "aJ": (48, I32),
    "w32": (4, I32), "th32": (4, I32), "thf": (4, F32),
    "inp": (160, BF), "inn": (144, F32), "ing": (128, BF), "pI": (8, I32), "col": (64, F32), "mask": (16, F32),
    "E0": (160, BF), "E1": (160, BF), "Id": (128, BF), "nId": (128, BF), "hId": (128, BF), "Big": (144, BF), "BigC": (144, BF),
    "BigN": (144, BF), "BigW": (432, BF), "BO": (128, BF), "BOd": (128, BF), "BOo": (128, BF),
    "mat": (1152, BF), "A3": (256, F32), "o16": (128, BF), "s8": (128, F32), "lP15": (16, U16), "lPerm": (16, U16), "tl": (48, F32),
    "pw": (32, F32), "thrB": (256, F32), "iB": (256, BF), "one": (512, BF), "jm": (256, BF), "diag": (256, BF), "segm": (256, BF),
    "pos": (64, F16), "seg": (64, F32), "nL": (48, F16), "nI": (48, F32), "scol": (8, F32), "junk": (320, BF), "jv": (640, BF),
    "Rs": (2048, BF), "Eg": (1024, BF), "cv": (768, F16), "cvn": (768, F32),
    "kvs": (768, F16), "kvd": (768, F16), "tr": (768, F32), "off1": (768, U16), "off2": (768, U16), "xv4": (3072, BF), "kC4": (3072, F16),
    "G": (8192, F16), "Cq": (8192, BF), "xc": (8192, BF), "ad": (8192, BF), "cW": (816, F32), "best": (192, F32), "td": (64, F32),
    "km": (16, I32), "wi": (16, I32), "wl": (16, U16), "nc": (16, BF), "Em": (256, F16), "mS": (256, F32), "mB": (256, F16),
    "wed": (320, BF), "cum": (320, BF), "Fv": (256, BF), "ms": (16, F32), "msl": (16, U16), "kmz": (256, F32), "Pr": (256, F16),
    "sm": (256, F16), "acc": (8, F32), "lan": (8, U16), "Dc": (64, U16), "xvc": (64, BF), "xvT": (128, BF), "xq": (1024, BF),
    "rs": (64, F32), "ri": (8, I32), "rj": (8, I32), "rl": (8, U16), "near": (64, BF), "zi": (8, I32), "thr": (8, F32),
    "eq": (4096, BF), "aq": (1024, BF), "kv2": (512, F16),
}
POOL = {}
for _p, _d, _names in (("poolf", F32, "ms acc thr scol td pw tl nI seg rs best"), ("pooli", I32, "aI aJ ri rj zi pI km wi"),
                       ("poolu", U16, "lP15 lPerm msl lan rl Dc wl")):
    _at = 0
    for _n in _names.split():
        POOL[_n] = (_p, _at)
        _at += (_S[_n][0] + 15) // 16 * 16
    _S[_p] = (_at, _d)
SCRATCH = {k: ("sbuf", [128, v[0]], v[1]) for k, v in _S.items() if k not in POOL}
SCRATCH["aq"] = ("sbuf", [128, 4, 256], BF)
SCRATCH["eq"] = ("sbuf", [128, 16, 256], BF)
SCRATCH["kv2"] = ("sbuf", [128, 2, 256], F16)
for _b in range(8):
    SCRATCH["P%d" % _b] = ("psum", [128, 512], F32)
_S["yk"] = (W, F32)
NDMA = 80
FLOWS = ["xs0", "xs1", "xs2", "a0", "a1", "a2", "d0", "d1", "d2", "xn01", "xn02", "xn12"]
SEMAPHORES = ["sV", "sA", "sP", "sG", "sent"] + ["m%d" % i for i in range(NDMA)] + FLOWS + ["h" + f for f in FLOWS]
SIZE = {F32: 4, BF: 2, F16: 2, I32: 4, U16: 2}
LAT = [3.5, 50e3]
CYC = 0.83e-3 * 1.25
PEC = 0.42e-3 * 1.25

BLOCKS = [
    [([0, 1, 2, 3], "VAVA", "aa", 1), ([4, 5, 6, 7], "VAVA", "bb", 1), ([8, 9, 10, 11], "AAAA", "aa", 4), ([12, 13, 14, 15], "AAAA", "ab", 4)],
    [([0, 1, 2, 3], "AAAA", "aa", 4), ([4, 9, 10, 11], "AAAA", "bb", 4), ([12, 13, 14, 15], "AAAA", "aa", 4), ([5, 8, 6, 7], "AAVA", "ab", 4)],
    [([0, 1, 2, 3], "AAAA", "aa", 4), ([9, 10, 11, 12], "AAAA", "aa", 4), ([13, 14, 15], "AAA", "bb", 4), ([4, 5, 8, 6, 7], "AAAVA", "aab", 4)],
]
CFG = {"mB": "AAA", "count": [0, 0, 2], "km": "AAA", "xq": ["AA", "AA", "AV"], "sm": "AAA", "mS": "VVV", "ncol": "VVV", "F": "VVV",
       "DS": "AAA", "kv2": "VA", "c": "A", "stride": True}


def flows(T):
    f = {}
    for t in range(R):
        f["xs%d" % t] = (t, "ans", ("X", 0, B), ("XQ%d" % t, 0, B))
        f["a%d" % t] = (t, "ask", ("aS", 16 * t, 16 * t + 16), ("aR%d" % t, 0, 16))
        f["d%d" % t] = (t, "ans", ("DS%d" % t, 0, L), ("D%d" % t, 0, L))
    for s, t in ((0, 1), (0, 2), (1, 2)):
        f["xn%d%d" % (s, t)] = (t, "ans", ("X", B + L * s, B + L * s + L), ("XQ%d" % t, B + L * s, B + L * s + L))
    return f


def route(T, topo, r, name):
    t, kind = flows(T)[name][:2]
    far = 1 + t % (N - 1)
    q = (r + far) % N if kind == "ask" else (r - far) % N
    src, dst = T.cores[r], T.cores[q]
    if topo.may_write(src, dst):
        return dst, None
    can = [c for c in topo.cores_of(src) if c != src and T.rank_of(c) is None and topo.may_write(c, dst)]
    same = [c for c in can if topo.die(c) == topo.die(src)]
    other = [c for c in can if topo.die(c) != topo.die(src)]
    if name.startswith("xs"):
        return dst, (same[0] if t == 0 else other[0])
    return dst, same[-1]


def nbits(m):
    return bin(m).count("1")


RELAY_ORDER = ["xs0", "a0", "a2", "xs2", "d0", "xn02", "d2", "xn12", "xs1", "a1", "d1", "xn01"]


def relay_program(g, core, T, topo):
    fl = flows(T)
    sent = 0
    for name in RELAY_ORDER:
        for r in range(N):
            dst, rel = route(T, topo, r, name)
            if rel != core:
                continue
            nm, lo, hi = fl[name][3]
            g.wait_ge(T.sem["h" + name], nbits(topo.mask(T.cores[r], core)))
            rid, pid = topo.addr(dst, core)
            m = topo.mask(core, dst)
            g.remote_dma(T[nm][:, lo:hi], T[nm][:, lo:hi], T.sem[name], T.sem.sent, pid, rid, m)
            sent += nbits(m)
    if sent:
        g.wait_ge(T.sem.sent, sent)


def meet(x, y):
    if x[0] >= y[1] or y[0] >= x[1]:
        return False
    return not (CFG["stride"] and x[2] == y[2] > 1 and (x[0] - y[0]) % x[2])


def runs(ks):
    out, u = [], 0
    for v in range(1, len(ks) + 1):
        if v == len(ks) or ks[v] != ks[v - 1] + 1:
            out.append((u, v))
            u = v
    return out


def rank_program(g, core, T, topo):
    rank = T.rank_of(core)
    if rank is None:
        return relay_program(g, core, T, topo)
    ops = []
    last = {}
    Q = {"V": g.vector, "A": g.scalar, "P": g.tensor, "G": g, "S": g.sync}

    def a(nm, lo=0, hi=None, st=1):
        psum = nm[0] == "P" and nm[1:].isdigit()
        if hi is None:
            hi = 512 if psum else _S[nm][0]
        if nm in POOL:
            nm, lo, hi = POOL[nm][0], lo + POOL[nm][1], hi + POOL[nm][1]
        ap = T[nm][:, lo:hi] if st == 1 else T[nm][:, lo:hi:st]
        n = len(range(lo, hi, st))
        if psum:
            return {"ap": ap, "r": [(nm, (0, 512, 1))], "n": n, "sz": 4, "ps": True}
        return {"ap": ap, "r": [(nm, (lo, lo + (n - 1) * st + 1, st))], "n": n, "sz": SIZE[_S[nm][1]], "ps": False}

    def view(ap, nm, lo, hi, n):
        return {"ap": ap, "r": [(nm, (lo, hi, 1))], "n": n, "sz": SIZE[_S[nm][1]], "ps": False}

    def ind(win, off):
        return {"ap": win["ap"].indirect(off["ap"]), "r": win["r"] + off["r"], "n": 16 * off["n"], "sz": win["sz"], "ps": False,
                "win": win["r"], "off": off["r"]}

    def op(eng, fn, reads, writes, cost, kind="c", after=(), wait=None):
        i = len(ops)
        deps = set(after)
        acc = []
        for x in reads:
            for r_ in x["r"]:
                acc.append((r_, x["ps"]))
        for x in writes:
            if "win" in x:
                acc += [(r_, True) for r_ in x["win"]] + [(r_, False) for r_ in x["off"]]
            else:
                acc += [(r_, True) for r_ in x["r"]]
        for (nm, cs), wr in acc:
            for (c2, j, w2) in last.get(nm, []):
                if (wr or w2) and meet(cs, c2):
                    deps.add(j)
        for (nm, cs), wr in acc:
            lst = last.setdefault(nm, [])
            if wr and cs[2] == 1:
                lst[:] = [e for e in lst if not (cs[0] <= e[0][0] and e[0][1] <= cs[1])]
            lst.append((cs, i, wr))
        deps.discard(i)
        typ = "x" if kind != "c" else "s" if any("win" in x for x in writes) else "g" if any("win" in x for x in reads) else "c"
        cost *= PLANF.get(typ, 1.0)
        ops.append({"e": eng, "typ": typ, "fn": fn, "deps": deps, "cost": cost, "kind": kind, "wait": wait})
        return i

    def vcost(ins, out, two=False):
        n = out["n"]
        if "win" in out:
            return 0.05 + n * 3.8 * CYC
        if any("win" in x for x in ins):
            return 0.05 + n * 1.56 * CYC
        rate = 2.0 if two else (0.5 if all(x["sz"] == 2 for x in ins + [out]) else 1.0)
        return 0.04 + max(64, n * rate) * CYC

    def val(s):
        return s["ap"] if isinstance(s, dict) else s

    def cols(*s):
        return [x for x in s if isinstance(x, dict)]

    def copy(o, i):
        return op("V", lambda q: q.tensor_copy(o["ap"], i["ap"]), [i], [o], vcost([i], o))

    def tt(o, i0, i1, f):
        return op("V", lambda q: q.tensor_tensor(o["ap"], i0["ap"], i1["ap"], f), [i0, i1], [o],
                  vcost([i0, i1], o, not (i0["ps"] or i1["ps"])))

    def ts(o, i, s1, f0, s2=None, f1=None):
        if f1 is None:
            fn = lambda q: q.tensor_scalar(o["ap"], i["ap"], val(s1), None, f0)
        else:
            fn = lambda q: q.tensor_scalar(o["ap"], i["ap"], val(s1), val(s2), f0, f1)
        return op("V", fn, [i] + cols(s1, s2), [o], vcost([i], o))

    def red(o, i):
        return op("V", lambda q: q.tensor_reduce(o["ap"], i["ap"], AxisListType.X, ALU.add), [i], [o], 0.04 + max(64, i["n"]) * CYC)

    def mset(o, c):
        return op("V", lambda q: q.memset(o["ap"], c), [], [o], vcost([], o))

    def scan(o, d0, d1, init, f0, f1):
        return op("V", lambda q: q.tensor_tensor_scan(o["ap"], d0["ap"], d1["ap"], init, f0, f1), [d0, d1], [o], vcost([d0, d1], o))

    def act(o, i, f=ACT.Identity, bias=0.0, scale=1.0, accum=None):
        if accum is None:
            fn = lambda q: q.activation(o["ap"], i["ap"], f, val(bias), val(scale))
        else:
            fn = lambda q: q.activation(o["ap"], i["ap"], f, val(bias), val(scale), accum_out=accum["ap"])
        c = 0.065 + (i["n"] * 1.56 if "win" in i else max(64, i["n"])) * CYC
        return op("A", fn, [i] + cols(bias, scale), [o] + cols(accum), c)

    def lin(eng, o, i, scale=None, bias=None):
        if eng == "G":
            return pick(o, i, [[0, o["n"]]], 0, 0)
        if eng == "A":
            return act(o, i, ACT.Identity, 0.0 if bias is None else bias, 1.0 if scale is None else scale)
        if scale is None and bias is None:
            return copy(o, i)
        if bias is None:
            return ts(o, i, scale, ALU.mult)
        if scale is None:
            return ts(o, i, bias, ALU.add)
        return ts(o, i, scale, ALU.mult, bias, ALU.add)

    def mm(lst, first=True, final=True):
        def fn(q):
            ins = None
            for j, (o, l_, r_) in enumerate(lst):
                ins = q.matmul(o["ap"], l_["ap"], r_["ap"], first and j == 0, final and j == len(lst) - 1)
            return ins
        c = sum(max(64, r_["n"]) * (4 if r_["sz"] == 4 else 1) for o, l_, r_ in lst) * PEC
        return op("P", fn, [x for e in lst for x in e[1:]], [e[0] for e in lst], c)

    def iota(o, pat, base, cm, flag=True):
        if flag:
            fn = lambda q: q.iota(o["ap"], pat, base, cm, allow_small_or_imprecise_dtypes=True)
        else:
            fn = lambda q: q.iota(o["ap"], pat, base, cm)
        return op("G", fn, [], [o], 0.13 + 2 * o["n"] * CYC)

    def pick(o, i, pat, base, cm):
        return op("G", lambda q: q.affine_select(o["ap"], i["ap"], pat, ALU.is_equal, 0.0, base, cm), [i], [o], 0.17 + 2 * o["n"] * CYC)

    def dma(eng, oap, iap, reads, writes, nbytes, after=()):
        return op(eng, lambda q: q.dma_start(oap, iap), reads, writes, 2.0 + nbytes / 150e3, "d", after)

    fl = flows(T)
    sent = [0]
    ARR = {}

    def send(name, after=()):
        t, kind, (sn, sl, sh), (dn, dl, dh) = fl[name]
        dst, rel = route(T, topo, rank, name)
        to = dst if rel is None else rel
        rid, pid = topo.addr(to, core)
        m = topo.mask(core, to)
        sem = T.sem[name] if rel is None else T.sem["h" + name]
        sent[0] += nbits(m)
        nb = 128 * (sh - sl) * SIZE[_S[sn][1]]
        s = op("G", lambda q: q.remote_dma(T[dn][:, dl:dh], T[sn][:, sl:sh], sem, T.sem.sent, pid, rid, m), [a(sn, sl, sh)], [], 0.3, "r", after)
        far = 1 + t % (N - 1)
        frm = (rank - far) % N if kind == "ask" else (rank + far) % N
        d2, r2 = route(T, topo, frm, name)
        cnt = nbits(topo.mask(T.cores[frm] if r2 is None else r2, core))
        lat = (LAT[0] + nb / LAT[1]) * (1 if rel is None else 2)
        ARR[name] = len(ops)
        op("X", None, [], [a(dn, dl, dh)], lat, "x", [s], (name, cnt))
        return s

    def top64(nm, lo, hi):
        return view(T[nm][0:64, lo:hi], nm, lo, hi, hi - lo)

    def eqp(b_, lo, hi):
        return view(T.eq[:, b_, lo:hi], "eq", 256 * b_ + lo, 256 * b_ + hi, hi - lo)

    at = {}

    def C(name, n=1):
        if name not in at:
            at[name] = sum(at.get("_n", []))
            at.setdefault("_n", []).append(n)
        return a("col", at[name], at[name] + n)

    def Ct(name, t):
        return a("col", at[name] + t, at[name] + t + 1)

    def M(j):
        return a("mask", j, j + 1)

    def mat(j):
        return a("mat", 128 * j, 128 * j + 128)

    def big(nm, a_, base=0):
        return a(nm, base + 15 - a_, base + 143 - a_)

    def kc_rows(lo, hi, src):
        js = [dma("S", T.KC[j:128:16, lo:hi], T[src][j:128:16, lo:hi], [a(src, lo, hi), a("KC", lo, hi)], [], 40e3) for j in range(6)]
        last["KC"] = [e for e in last["KC"] if e[1] not in js] + [((lo, hi, 1), j, True) for j in js]

    dma("S", T.kin32[:, 0:576], T.kin[:, 0:576], [], [a("kin32", 0, 576)], 300e3)
    dma("A", T.kin32[:, 576:B], T.kin[:, 576:B], [], [a("kin32", 576, B)], 300e3)
    dma("S", T.X[:, 0:B], T.xf[:, :], [], [a("X", 0, B)], 500e3)
    dma("A", T.w32[:, 0:3], T.w[:, :], [], [a("w32", 0, 3)], 0)
    dma("S", T.th32[0:8, 0:3], T.th[:, :], [], [a("th32", 0, 3)], 0)

    iota(a("pI", 0, 1), [[1, 1]], 0, 1, False)
    iota(a("inp"), [[1, 160]], -16, -1)
    iota(a("inn"), [[1, 144]], 0, 0)
    ts(a("pI", 1, 2), a("pI", 0, 1), 15, ALU.bitwise_and)
    ts(a("pI", 2, 3), a("pI", 0, 1), 112, ALU.bitwise_and)
    ts(a("pI", 3, 4), a("pI", 0, 1), 16, ALU.bitwise_and)
    copy(C("p", 3), a("pI", 1, 4))
    row, g16, odd16 = Ct("p", 0), Ct("p", 1), Ct("p", 2)
    ts(C("end"), g16, 15.0, ALU.add)
    ts(C("odd"), odd16, 0.0625, ALU.mult)
    ts(C("even"), odd16, 0.0, ALU.is_equal)
    ts(a("E0"), a("inp"), 0.0, ALU.is_equal, C("even"), ALU.mult)
    ts(a("E1"), a("inp"), 0.0, ALU.is_equal, C("odd"), ALU.mult)
    ts(a("mask"), a("inn", 0, 16), row, ALU.is_equal)
    ts(a("Big"), a("inn"), C("end"), ALU.is_equal)
    ts(C("r16"), row, 16.0, ALU.mult)
    ts(a("lPerm"), a("inn", 0, 16), C("r16"), ALU.add)
    sq = a("inp", 16, 144)
    ts(a("Id"), sq, 0.0, ALU.is_equal)
    act(a("nId"), a("Id"), scale=-1.0)
    act(a("BigC"), a("Big"), scale=BIGK)
    act(a("BigN"), a("Big"), scale=-512.0)
    iota(a("KC", 0, B), [[0, B // 4], [1, 4]], 0, 0)
    iota(a("iB"), [[1, 256]], 0, 0)
    mset(a("one"), 1.0)

    def first_lists(t, bank):
        lin("G" if t else "V", a("kvs", 256 * t, 256 * t + 256), a("kin32", t, 1024, 4))
        for bp in range(8):
            for c in range(2):
                o = a(bank, 32 * bp + 16 * c, 32 * bp + 16 * c + 16)
                e = "E%d" % c
                lst = []
                for x in range(2):
                    sh = 16 - 16 * (x - c)
                    b_ = 2 * bp + x
                    lst.append((o, a(e, sh, sh + 128), a("kvs", 256 * t + 16 * b_, 256 * t + 16 * b_ + 16)))
                mm(lst)
        o, i = a("tr", 256 * t, 256 * t + 256), a(bank, 0, 256)
        op("V", lambda q: q.transpose(o["ap"], i["ap"]), [i], [o], vcost([i], o))
        copy(a("off1", 256 * t, 256 * t + 256), ind(o, a("lPerm")))

    def repeat(nm, t):
        for j in range(1, 4):
            lo = 1024 * t + 256 * j
            dma("S", T[nm][:, lo:lo + 256], T[nm][:, 1024 * t:1024 * t + 256], [a(nm, 1024 * t, 1024 * t + 256)], [a(nm, lo, lo + 256)], 65e3)

    def suitors(t):
        lin("G", a("xv4", 1024 * t, 1024 * t + 256), a("X", t, 1024, 4))
        repeat("xv4", t)
        lin("G", a("kC4", 1024 * t, 1024 * t + 256), a("KC", t, 1024, 4))
        repeat("kC4", t)

    def own_features(t):
        n0 = B + L * t
        dma("S", T.X[:, n0:n0 + 320], T.xv4[:, 1024 * t:1024 * t + 320], [a("xv4", 1024 * t, 1024 * t + 320)], [a("X", n0, n0 + 320)], 80e3)

    first_lists(0, "P6")
    copy(a("K0f", 0, 576), a("kin32", 0, 576))
    copy(a("K0f", 576, B), a("kin32", 576, B))
    kc_rows(0, B, "K0f")
    suitors(0)

    copy(C("w", 3), a("w32", 0, 3))
    for t in range(R):
        act(a("BigW", 144 * t, 144 * t + 144), a("Big"), scale=Ct("w", t))
        mm([(a("P7", 16 * t, 16 * t + 16), big("BigW", a_, 144 * t), a("X", 4 * a_ + t, 1024, 64)) for a_ in range(16)])
    copy(a("aI"), a("P7", 0, 48))
    ts(a("aJ"), a("aI"), 1023, ALU.bitwise_and)
    copy(a("aS"), a("aJ"))
    s0 = send("xs0")
    s1 = send("a0", [s0])
    s1 = send("a1", [s1])
    s1 = send("a2", [s1])
    dma("S", T.Kf[:, 0:B], T.K0f[:, :], [a("K0f")], [a("Kf", 0, B)], 600e3, [ARR["a0"]])
    own_features(0)

    iota(a("ing"), [[16, 8], [0, 16]], 0, 0)
    iota(a("jm"), [[0, 16], [1, 16]], 0, 0)
    iota(a("KC", B, W), [[0, (W - B) // 4], [1, 4]], 0, 0)
    ts(a("BO"), a("ing"), g16, ALU.is_equal)
    act(a("BOo"), a("BO"), scale=65536.0)
    ts(a("diag"), a("jm"), row, ALU.is_equal)
    ts(a("segm"), a("jm"), 0.0, ALU.is_gt)
    ts(a("seg"), a("jm", 0, 64), 0.0, ALU.is_equal, 8388608.0, ALU.mult)
    for q_ in range(4):
        pick(a("Rs", 512 * q_, 512 * q_ + 512), a("one"), [[-1, 4], [-16, 8], [0, 16]], -4 * q_, 1)
    for h in range(2):
        pick(top64("Eg", 512 * h, 512 * h + 512), top64("one", 0, 512), [[-1, 32], [0, 16]], -32 * h, 1)
    mset(a("o16"), 0.0625)
    iota(a("wed", 256, 320), [[0, 64]], 0, 0)
    ts(a("lP15"), a("inn", 0, 16), 0.0, ALU.mult, row, ALU.add)
    mset(a("tl", 0, 16), 0.5)
    mset(a("tl", 16, 32), 0.0)
    scan(a("pw", 0, 16), a("tl", 0, 16), a("tl", 16, 32), 131072.0, ALU.mult, ALU.add)
    copy(a("thrB"), ind(a("pw", 0, 16), a("lP15")))
    ts(a("tl", 16, 32), a("mask"), 0.5, ALU.mult)
    tt(a("pw", 16, 32), a("pw", 0, 16), a("tl", 16, 32), ALU.mult)
    red(C("pw"), a("pw", 16, 32))
    act(a("BOd"), a("BO"), scale=C("pw"))
    iota(a("nI"), [[L, R], [16, 16]], B, 0)
    ts(a("nL"), a("nI"), row, ALU.add)
    for t in range(R):
        iota(a("D%d" % t, 256, 320), [[0, 64]], 0, 0)
        iota(a("cW", 272 * t + 256, 272 * t + 272), [[0, 16]], -1, 0)
    iota(a("rs"), [[256, 4], [1, 16]], 0, 0)
    ts(a("pos"), a("rs"), C("r16"), ALU.add)
    ts(a("scol", 0, 4), a("inn", 0, 64, 16), row, ALU.add, -0.5, ALU.add)
    act(a("hId"), a("Id"), scale=0.5)
    t3 = a("inn", 0, 3)
    ts(C("lt2"), row, 2.0, ALU.is_lt)
    ts(C("lt9"), row, 9.0, ALU.is_lt)
    ts(C("r911"), row, 12.0, ALU.is_lt, C("lt9"), ALU.subtract)
    ts(C("m67"), M(6), M(7), ALU.add)
    ts(C("n67"), C("m67"), -1.0, ALU.mult, 1.0, ALU.add)
    ts(C("d5"), C("m67"), C("r911"), ALU.add)
    ts(C("s1a"), C("lt2"), 2.0, ALU.mult, M(7), ALU.add)
    ts(C("s1"), M(6), 6.0, ALU.mult, C("s1a"), ALU.add)
    ts(C("w1"), C("lt2"), M(7), ALU.add, M(6), ALU.subtract)
    ts(mat(0), sq, C("s1"), ALU.is_equal, C("w1"), ALU.mult)
    act(mat(1), a("nId"), scale=C("d5"))
    ts(C("m1c"), M(1), M(12), ALU.add)
    act(mat(2), a("Id"), scale=C("m1c"))
    ts(a("A3", 0, 128), sq, 4.0, ALU.is_equal, C("lt2"), ALU.mult)
    act(a("A3", 128, 256), a("nId"), scale=C("lt9"))
    tt(a("A3", 0, 128), a("A3", 0, 128), a("A3", 128, 256), ALU.add)
    act(mat(3), a("Id"), scale=C("lt9"))
    act(mat(4), a("Id"), scale=C("m67"))
    ts(C("s6"), M(12), -6.0, ALU.mult)
    ts(C("w6"), M(12), M(7), ALU.add, C("r911"), ALU.add)
    ts(mat(5), sq, C("s6"), ALU.is_equal, C("w6"), ALU.mult)
    ts(C("w7"), C("r911"), -1001.0, ALU.mult, 1.0, ALU.add)
    act(mat(6), a("Id"), scale=C("w7"))
    act(mat(7), a("nId"), scale=C("r911"))
    ts(C("f0"), C("r911"), 4999.5, ALU.mult, 0.5, ALU.add)
    ts(C("f", 3), a("mask", 9, 12), -5063.5, ALU.mult, C("f0"), ALU.add)
    ts(C("ca"), M(0), 4.0, ALU.mult, C("d5"), ALU.add)
    ts(C("cb1"), C("d5"), float(L), ALU.mult, M(0), ALU.add)
    ts(C("cb0"), C("d5"), float(B), ALU.mult)
    ts(C("cb", 3), t3, C("cb1"), ALU.mult, C("cb0"), ALU.add)
    ts(C("cc"), M(6), 4.0, ALU.mult, M(7), ALU.add)
    ts(C("cd1"), M(7), float(L), ALU.mult, M(6), ALU.add)
    ts(C("cd0"), M(7), float(B), ALU.mult)
    ts(C("cd", 3), t3, C("cd1"), ALU.mult, C("cd0"), ALU.add)
    for t in range(R):
        lin("V", a("cv", 256 * t, 256 * t + 256), a("iB"), C("ca"), Ct("cb", t))
        lin("A", a("cvn", 256 * t, 256 * t + 256), a("iB"), C("cc"), Ct("cd", t))
    s8 = view(T.s8[0:8, :], "s8", 0, 128, 128)
    iota(s8, [[1, 8], [0, 16]], 0, -1)
    ts(s8, s8, 0.0, ALU.is_equal, 512.0, ALU.mult)
    thf = view(T.thf[0:8, 0:3], "thf", 0, 3, 3)
    ts(thf, view(T.th32[0:8, 0:3], "th32", 0, 3, 3), 4081.0, ALU.min)
    mm([(a("P7", 64, 67), s8, thf)])
    copy(C("th", 3), a("P7", 64, 67))

    def scores(t, s0, block, late, banks):
        ks, l1, how, kw = block
        bd0, bd1, bc, bk = banks
        n = len(ks)
        P = B + L * t if late else B
        base = 4096 * (t & 1) + 256 * s0
        o1, o2 = 256 * t, 256 * t + 16 * s0

        def part(nm, u, v):
            return a(nm, base + 256 * u, base + 256 * v)

        def turn(o, w_, nm, u, v):
            return [(o, big(w_, a_), a(nm, base + 256 * u + a_, base + 256 * v, 16)) for a_ in range(16)]

        for u, v in ([(0, n - 2), (n - 2, n)] if late else [(0, n)]):
            for s_ in range(u, v):
                k = ks[s_]
                win = a("Kf", 0, P) if late else a("kin32" if l1[s_] == "V" else "K0f")
                lin(l1[s_], part("G", s_, s_ + 1), ind(win, a("off1", o1 + 16 * k, o1 + 16 * k + 16)), M((k + t) & 15))
            mm(turn(a(bc, 0, 16 * (v - u)), "Big", "G", u, v))
            copy(a("off2", o2 + 16 * u, o2 + 16 * v), a(bc, 0, 16 * (v - u)))
            for x, y in runs(ks[u:v]):
                k = ks[u + x]
                lin(CFG["c"], a("cW", 272 * t + 16 * k, 272 * t + 16 * (k + y - x)), a(bc, 16 * x, 16 * y))
            for x in range(u, v, kw):
                y = min(x + kw, v)
                tt(part("Cq", x, y), ind(a("KC", 0, P), a("off2", o2 + 16 * x, o2 + 16 * y)),
                   a("kC4", 1024 * t, 1024 * t + 256 * (y - x)), ALU.is_equal)
        mm(turn(a(bk, 0, 16 * n), "BigC", "Cq", 0, n)
           + [(a(bk, 16 * u, 16 * v), a("Id"), a("iB", 16 * ks[u], 16 * (ks[u] + v - u))) for u, v in runs(ks)], True, False)
        cuts = [max(0, n - 2 * j) for j in range(len(how), -1, -1)]
        pairs = list(zip(cuts, cuts[1:], how))
        same = [[pairs[0]]]
        for p_ in pairs[1:]:
            if p_[2] == same[-1][0][2]:
                same[-1].append(p_)
            else:
                same.append([p_])
        xv = a("xv4", 1024 * t, 1024 * t + 256)
        for j, grp in enumerate(same):
            u, v = grp[0][0], grp[-1][1]
            o = a(bk, 16 * u, 16 * v)
            end = j == len(same) - 1
            if grp[0][2] == "a":
                for x, y, _ in grp:
                    bank = (bd0, bd1)[(n - x) // 2 & 1]
                    w_ = 256 * (y - x)
                    act(part("xc", x, y), ind(a("X", 0, P), a("off2", o2 + 16 * x, o2 + 16 * y)))
                    mm([(a(bank, 256 * z, 256 * z + 256), a("nId"), xv) for z in range(y - x)] + [(a(bank, 0, w_), a("Id"), part("xc", x, y))])
                    act(part("ad", x, y), a(bank, 0, w_), ACT.Abs, scale=512.0)
                mm(turn(o, "Big", "ad", u, v), False, end)
            else:
                for x in range(u, v, kw):
                    y = min(x + kw, v)
                    tt(part("ad", x, y), ind(a("X", 0, P), a("off2", o2 + 16 * x, o2 + 16 * y)),
                       a("xv4", 1024 * t, 1024 * t + 256 * (y - x)), ALU.subtract)
                ts(part("xc", u, v), part("ad", u, v), 0.0, ALU.max, -2.0, ALU.mult)
                mm(turn(o, "BigN", "ad", u, v), False, False)
                mm(turn(o, "BigN", "xc", u, v), False, end)

    def least(t, j, bank):
        n = len(BLOCKS[t][j][0])
        w_ = 16 * min(n, 4)
        b_ = a("best", 64 * t, 64 * t + w_)
        if j == 0:
            ts(b_, a(bank, 0, w_), NONE, ALU.min)
        else:
            tt(b_, a(bank, 0, w_), b_, ALU.min)
        if j == len(BLOCKS[t]) - 1:
            tt(a("td", 0, 32), a("best", 64 * t, 64 * t + 32), a("best", 64 * t + 32, 64 * t + 64), ALU.min)
            if n > 4:
                tt(a("td", 0, 16), a(bank, 64, 80), a("td", 0, 16), ALU.min)
            tt(a("km"), a("td", 0, 16), a("td", 16, 32), ALU.min)

    def late_lists(t):
        for j in range(2):
            lin(CFG["kv2"][j], view(T.kv2[:, j, :], "kv2", 256 * j, 256 * j + 256, 256), a("Kf", t, 1024, 4), M(6 + j))
        mm([(a("P6", 0, 32), big("Big", a_), view(T.kv2[:, :, a_:256:16], "kv2", 0, 512, 32)) for a_ in range(16)])
        copy(a("off1", 256 * t + 96, 256 * t + 128), a("P6", 0, 32))

    SB = ("P0", "P0", "P2", "P3")

    def static_part(t):
        for j in range(3):
            banks = SB if t else (("P0", "P1", "P2", "P3"), ("P4", "P5", "P6", "P7"))[j & 1]
            scores(t, 4 * j, BLOCKS[t][j], False, banks)
            least(t, j, banks[3])

    def dynamic_part(t):
        n0 = B + L * t
        lastr = t == R - 1
        lin(CFG["DS"][t], a("DS%d" % t), ind(a("Kf" if t else "K0f", 0, 1024), a("aR%d" % t)))
        sd = send("d%d" % t)
        if t == 0:
            send("xs2", [sd])
            send("xs1", [sd])
            kv = a("kvs", 0, 256)
            thr = Ct("th", 0)
        else:
            kv = a("kvd", 256 * t, 256 * t + 256)
            lin("G", kv, a("Kf", t, 1024, 4))
            thr = a("thr", t, t + 1)
        lin("G", a("Kf", n0, n0 + L), a("Kf", t, 1024, 4))
        s0 = sum(len(b_[0]) for b_ in BLOCKS[t][:3])
        scores(t, s0, BLOCKS[t][3], t > 0, ("P4", "P5", "P7", "P7") if t else ("P4", "P5", "P6", "P7"))
        least(t, 3, "P7")
        ts(a("wi"), a("km"), 511, ALU.bitwise_and)
        copy(a("wl"), a("wi"))
        ts(a("nc"), a("km"), thr, ALU.is_ge, 65536.0, ALU.mult)
        tt(a("Em"), ind(a("cW", 272 * t, 272 * t + 272), a("wl")), a("diag"), ALU.mult)
        mm([(a("P5", 0, 256), a("BO"), a("Em"))])
        lin(CFG["mB"][t], a("mB"), a("P5", 0, 256))
        mS = a("mS", 15, 256, 16)
        if CFG["mS"][t] == "V":
            scan(a("mS"), a("segm"), a("Em"), 0.0, ALU.mult, ALU.add)
        else:
            mm([(a("P6", 0, 16), a("Id"), a("Em", a_, 256, 16)) for a_ in range(16)])
            act(mS, a("P6", 0, 16))
        mm([(a("P7", a_, 256, 16), a("Rs", 128 * a_, 128 * a_ + 128), a("nc")) for a_ in range(16)], True, False)
        for b_ in range(16):
            ts(eqp(b_, 0, 256 - 16 * b_), a("mB", 16 * b_, 256), a("mS", 16 * b_ + 15, 16 * b_ + 16), ALU.is_equal)
            if b_ < 15:
                mm([(a("P7", 16 * b_ + 16, 256), a("BOo"), eqp(b_, 16, 256 - 16 * b_))], False, False)
        mm([(a("P7", 0, 256), a("BOd"), view(T.eq[:, :, 0:16], "eq", 0, 4096, 256))], False, True)
        mm([(a("P4", 0, 256), l_, r_) for l_, r_ in ((mat(0), kv), (mat(1), kv), (mat(2), a("mB")), (a("Id"), a("cv", 256 * t, 256 * t + 256)))], True, False)
        wed = a("wed", 0, 256)
        tt(wed, a("P7", 0, 256), a("thrB"), ALU.is_lt)
        mm([(a("P6", 0, 16), a("Id"), a("nL", 16 * t, 16 * t + 16))] + [(a("P6", 0, 16), big("BigN", a_), a("wed", a_, 256, 16)) for a_ in range(16)])
        scan(a("cum"), a("one", 0, 320), a("wed"), -1.0, ALU.add, ALU.subtract)
        tt(a("ms"), a("P6", 0, 16), mS, ALU.max)
        copy(a("msl"), a("ms"))
        nv = CFG["count"][t]
        for c in range(nv):
            ts(a("jv", 320 * c, 320 * c + 320), a("cum"), a("scol", c, c + 1), ALU.is_lt, 0.5, ALU.subtract)
            red(a("acc", c, c + 1), a("jv", 320 * c, 320 * c + 320))
        for c in range(nv, 4):
            lo = 16 if c in (1, 2) else 0
            act(a("junk", lo, 320 - lo), a("cum", lo, 320 - lo), ACT.Sign, a("scol", c, c + 1), -1.0, a("acc", c, c + 1))
        lin(CFG["km"][t], a("kmz"), ind(a("Kf", 0, n0 + L), a("msl")), C("n67"))
        mm([(a("P5", 0, 256), mat(6), wed), (a("P5", 0, 256), mat(7), a("cum", 0, 256))])
        ts(a("Fv"), a("P5", 0, 256), Ct("f", t), ALU.is_gt)
        mm([(a("P4", 0, 256), a("A3", 0, 128), a("kmz"))], False, True)
        tt(ind(a("Kf", 0, n0 + L), a("msl")), a("kmz"), a("cvn", 256 * t, 256 * t + 256), ALU.add)
        if not lastr:
            late_lists(t + 1)
        tt(a("Pr"), a("P4", 0, 256), a("Fv"), ALU.mult)
        mm([(a("P7", 0, 256), mat(4), kv), (a("P7", 0, 256), mat(3), a("Pr"))])
        mm([(a("P4", 0, 256), a("Id"), kv), (a("P4", 0, 256), mat(5), a("Pr"))])
        tt(a("Kf", n0, n0 + L), a("P7", 0, 256), a("kmz"), ALU.add)
        act(a("Kf", t, 1024, 4), a("P4", 0, 256))
        if not lastr:
            kc_rows(n0, n0 + L, "Kf")
        if t == 0:
            dma("S", T.yk[:, 0:B], T.K0f[:, :], [a("K0f")], [a("yk", 0, B)], 600e3, [ARR["xs2"], ARR["xs1"]])
        dma("S", T.yk[:, n0:n0 + L], T.Kf[:, n0:n0 + L], [a("Kf", n0, n0 + L)], [a("yk", n0, n0 + L)], 130e3)
        if t:
            for r_ in ((9, 10), (6, 7, 11))[t - 1]:
                hi = n0 if r_ < 9 else 1024
                dma("S", T.yk[r_:128:16, 0:hi], T.Kf[r_:128:16, 0:hi], [a("Kf", 0, hi), a("yk", 0, hi)], [], 60e3)
        lin(CFG["sm"][t], a("sm"), ind(a("X", 0, n0 + L), a("msl")), None, -0.5)
        mm([(a("P5", 256, 512), a("hId"), r_) for r_ in (a("xv4", 1024 * t, 1024 * t + 256), a("sm"))])
        ts(a("X", n0, n0 + L), a("P5", 256, 512), MAGIC, ALU.add, MAGIC, ALU.subtract)
        if nv:
            ts(a("lan", 0, nv), a("acc", 0, nv), 160.0, ALU.add)
        if nv < 4:
            ts(a("lan", nv, 4), a("acc", nv, 4), 0.5, ALU.mult, 160.0, ALU.add)
        lan = a("lan", 0, 4)
        copy(a("Dc"), ind(a("D%d" % t), lan))
        act(a("xvc"), ind(a("xv4", 1024 * t, 1024 * t + 320), lan))
        xqw = a("XQ%d" % t)
        b0, b1, b2 = ("P1", "P0", "P2") if lastr else ("P1", "P5", "P6")
        pt = {"ap": T[b0][0:64, 0:128], "r": [(b0, (0, 512, 1))], "n": 128, "sz": 4, "ps": True}
        mm([(pt, a("xvc"), a("nId"))])
        act(top64("xvT", 0, 128), pt)
        for h, bank in enumerate((b0, b1)):
            mm([(a(bank), top64("xvT", 0, 128), top64("Eg", 512 * h, 512 * h + 512))], True, False)
            xq = a("xq", 512 * h, 512 * h + 512)
            lin(CFG["xq"][t][h], xq, ind(xqw, a("Dc", 32 * h, 32 * h + 32)))
            mm([(a(bank), a("Id"), xq)], False, True)
            act(view(T.aq[:, 2 * h:2 * h + 2, :], "aq", 512 * h, 512 * h + 512, 512), a(bank), ACT.Abs, scale=1024.0)
        o = a(b2, 0, 64)
        mm([(o, a("Id"), a("pos"))] + [(o, big("Big", a_), view(T.aq[:, :, 16 * a_:16 * a_ + 16], "aq", 0, 1024, 64)) for a_ in range(16)])
        scan(a("rs"), a("seg"), o, 0.0, ALU.add, ALU.min)
        copy(a("ri", 0, 4), a("rs", 15, 64, 16))
        ts(a("rj", 0, 4), a("ri", 0, 4), 1023, ALU.bitwise_and)
        copy(a("rl", 0, 4), a("rj", 0, 4))
        copy(a("near"), ind(a("xq"), a("rl", 0, 4)))
        copy(ind(a("X", n0, n0 + 320), lan), a("near"))
        if t == 0:
            send("xn02", [send("xn01")])
        if t == 1:
            send("xn12")
        dma("S", T.yx[:, L * t:L * t + L], T.X[:, n0:n0 + L], [a("X", n0, n0 + L)], [], 65e3)
        if not lastr:
            own_features(t + 1)
            mm([(a("P4", 0, 1), a("o16"), a("cum", 255, 256))])
            ts(a("zi", 0, 1), a("P4", 0, 1), -1.0, ALU.mult, 2040.0, ALU.add)
            ts(a("zi", 1, 2), a("zi", 0, 1), 15, ALU.bitwise_and)
            ts(a("thr", t + 1, t + 2), a("zi", 1, 2), 512.0, ALU.mult, Ct("th", t + 1), ALU.add)

    static_part(0)
    for t in range(R):
        if t < R - 1:
            suitors(t + 1)
            first_lists(t + 1, "P2")
        dynamic_part(t)
        if t < R - 1:
            static_part(t + 1)

    emit(ops, Q, T, sent[0])


LOG = []
PLAN = []
ITER, NOISE = [3000], [0.5, 2.0, 4.0, 8.0, 14.0]
PLANF = {"c": 0.9, "g": 0.85, "s": 0.9}
LAG = [0.3, 0.12]
SCALES = [{"l": 0.55, "c": 0.82, "g": 0.62, "s": 0.6, "x": 0.8}, {"l": 0.7, "c": 0.85, "g": 0.82, "s": 0.85, "x": 0.9},
          {"l": 0.55, "c": 1.0, "g": 1.0, "s": 1.0, "x": 1.0}, {"l": 0.55, "c": 1.16, "g": 1.45, "s": 1.6, "x": 1.0}]


def emit(ops, Q, T, sent):
    n = len(ops)
    succ = [[] for _ in ops]
    for i, o in enumerate(ops):
        for d in o["deps"]:
            succ[d].append(i)

    def lag(d, i):
        if ops[d]["e"] == ops[i]["e"]:
            return 0.0 if ops[d]["e"] == "P" else LAG[1]
        return LAG[0]

    def hold(i):
        o = ops[i]
        return 0.0 if o["e"] == "X" else (0.1 if o["kind"] == "d" else o["cost"])

    def place(seq, pre, back):
        st = [0.0] * n
        busy = {e: [] for e in "VAPGSX"}
        for i in seq:
            c, h = ops[i]["cost"], hold(i)
            t = 0.0
            for d in pre[i]:
                x = st[d] + ops[d]["cost"] + lag(d, i)
                if x > t:
                    t = x
            off = c - h if back else 0.0
            t += off
            lst = busy[ops[i]["e"]]
            k = len(lst)
            while k > 0 and lst[k - 1][1] > t:
                k -= 1
            while k < len(lst) and lst[k][0] < t + h:
                t = max(t, lst[k][1])
                k += 1
            if h:
                lst.insert(k, (t, t + h))
            st[i] = t - off
        return st

    def replay(order, scale):
        fin = [0.0] * n
        free = {e: 0.0 for e in "VAPGSX"}
        for i in order:
            o = ops[i]
            t = free[o["e"]] if o["e"] != "X" else 0.0
            for d in o["deps"]:
                t = max(t, fin[d] + lag(d, i) * scale["l"])
            f = scale[o["typ"]] / PLANF.get(o["typ"], 1.0)
            fin[i] = t + o["cost"] * f
            free[o["e"]] = t + hold(i) * f
        return max(fin)

    if not PLAN:
        pre = [list(o["deps"]) for o in ops]
        pr = [0.0] * n
        for i in range(n - 1, -1, -1):
            pr[i] = ops[i]["cost"] + max([pr[j] + lag(i, j) for j in succ[i]] or [0.0])
        seq = sorted(range(n), key=lambda i: (-pr[i], i))
        best, rnd = None, 12345
        for it in range(ITER[0]):
            st = place(seq, pre, False)
            order = sorted(range(n), key=lambda i: (st[i], i))
            vals = [replay(order, sc) for sc in SCALES]
            val = sum(math.log(v) for v in vals)
            if best is None or val < best[0]:
                best = (val, order, st, vals, max(pr))
            base = st if it % 4 else best[2]
            seq = sorted(range(n), key=lambda i: (-(base[i] + ops[i]["cost"]), -i))
            bt = place(seq, succ, True)
            key = [0.0] * n
            for i in range(n):
                rnd = (rnd * 1103515245 + 12345) % 2147483648
                key[i] = -(bt[i] + ops[i]["cost"]) + (rnd / 2147483648.0) * NOISE[it // 4 % len(NOISE)] * (it % 4 == 0)
            for i in range(n):
                for d in pre[i]:
                    key[i] = max(key[i], key[d] + 1e-6)
            seq = sorted(range(n), key=lambda i: (key[i], i))
        PLAN.append(best)
    order = list(range(5)) + [i for i in PLAN[0][1] if i >= 5]
    for i in range(n):
        ops[i]["t"] = (PLAN[0][2][i], PLAN[0][2][i] + ops[i]["cost"])
    cnt = {}
    known = {e: {} for e in "VAPGS"}
    nd = 0
    total = {}
    for i in order:
        o = ops[i]
        e = o["e"]
        if e == "X":
            o["done"] = {o["wait"][0]: o["wait"][1]}
            o["tok"] = o["wait"]
            total[o["wait"][0]] = o["wait"][1]
            continue
        kn = known[e]
        need = {}
        for d in o["deps"]:
            od = ops[d]
            if od["kind"] == "r" or (e == "P" and od["e"] == "P"):
                continue
            s, v = od["tok"]
            if kn.get(s, 0) < v:
                need[s] = max(need.get(s, 0), v)
        for d in o["deps"]:
            for s, v in ops[d].get("done", {}).items():
                if ops[d]["kind"] != "r" and not (e == "P" and ops[d]["e"] == "P") and ops[d]["tok"][0] != s and need.get(s, 0) and need[s] <= v:
                    need[s] = 0
        for s, v in need.items():
            if v:
                Q[e].wait_ge(T.sem[s], v)
        for d in o["deps"]:
            od = ops[d]
            if od["kind"] == "r" or (e == "P" and od["e"] == "P"):
                continue
            for s, v in od["done"].items():
                kn[s] = max(kn.get(s, 0), v)
        ins = o["fn"](Q[e])
        if o["kind"] == "r":
            continue
        if o["kind"] == "d":
            s, v = "m%d" % nd, 16
            nd += 1
            ins.then_inc(T.sem[s], 16)
        else:
            s = "s" + e
            v = cnt[s] = cnt.get(s, 0) + 1
            ins.then_inc(T.sem[s], 1)
        o["tok"] = (s, v)
        o["done"] = dict(kn)
        o["done"][s] = v
        total[s] = v
    for s, v in total.items():
        if max(known[e].get(s, 0) for e in known) < v:
            Q["S"].wait_ge(T.sem[s], v)
    Q["G"].wait_ge(T.sem.sent, sent)
    LOG[:] = [ops, order]
